import numpy as np
import ml_dtypes


def mxq(x, axis, fmt="e4m3"):
    dtype, down = {"e4m3": (ml_dtypes.float8_e4m3fn, 7), "e5m2": (ml_dtypes.float8_e5m2, 14)}[fmt]
    v = np.moveaxis(np.asarray(x, np.float32).astype(ml_dtypes.bfloat16).astype(np.float64), axis, -1)
    blocks = v.reshape(v.shape[:-1] + (-1, 32))
    amax = np.abs(blocks).max(-1, keepdims=True)
    byte = np.maximum(np.where(amax > 0, np.frexp(amax)[1] - 1 + 127, 0) - down, 1)
    scale = np.exp2(byte - 127.0)
    codes = (blocks / scale).astype(np.float32).astype(dtype).astype(np.float64)
    return np.moveaxis((codes * scale).reshape(v.shape), -1, axis)


WIDE = False


def mx_kscale(k):
    if not WIDE:
        return np.ones(k)
    levels = np.array([10, -10, 5, -5, 0])
    if k % 512:
        return np.exp2(np.random.permutation(np.resize(levels, k // 32))).repeat(32)
    a = np.empty((k // 512, 16))
    for p in range(k // 512):
        a[p, :8] = np.random.permutation(np.resize(levels, 8))
        for g in range(8):
            far = levels[np.abs(levels - a[p, g]) >= 10]
            a[p, g + 8] = far[np.random.randint(len(far))]
    return np.exp2(a.ravel()).repeat(32)


BF16 = ml_dtypes.bfloat16


def bf(x):
    return np.asarray(x, np.float32).astype(BF16)


def f64(x):
    return np.asarray(x).astype(np.float64)


E2M1 = np.array([0.0, 0.5, 1.0, 1.5, 2.0, 3.0, 4.0, 6.0, -0.0, -0.5, -1.0, -1.5, -2.0, -3.0, -4.0, -6.0])


def pack_weight(w, fmt):
    k, n = w.shape
    w = f64(bf(w)).reshape(k // 32, 32, n)
    amax = np.abs(w).max(1)
    if fmt == "e4m3":
        byte = np.frexp(amax)[1] - 1 + 127 - 7
    else:
        mant, ex = np.frexp(amax / 6.0)
        byte = np.where(mant > 0.5, ex, ex - 1) + 127
    byte = np.clip(np.where(amax > 0, byte, 1), 1, 254)
    scaled = (w * np.exp2(127.0 - byte)[:, None, :]).reshape(k, n).astype(np.float32)
    by_word = np.ascontiguousarray(scaled.reshape(k // 512, 128, 4, n).transpose(0, 1, 3, 2))
    if fmt == "e4m3":
        words = by_word.astype(ml_dtypes.float8_e4m3fn).view(np.uint8)
    else:
        c = by_word.astype(ml_dtypes.float4_e2m1fn).view(np.uint8) & 0xF
        words = c[..., 0::2] | (c[..., 1::2] << 4)
    return np.ascontiguousarray(words), np.ascontiguousarray(byte.astype(np.uint8).reshape(k // 512, 16, n))


def unpack_weight(words, scales, fmt):
    g, p, n, _ = words.shape
    if fmt == "e4m3":
        vals = np.ascontiguousarray(words).view(ml_dtypes.float8_e4m3fn).astype(np.float64)
    else:
        nib = np.empty((g, p, n, 4), np.uint8)
        nib[..., 0::2] = words & 0xF
        nib[..., 1::2] = words >> 4
        vals = E2M1[nib]
    vals = vals * np.repeat(np.exp2(scales.astype(np.float64) - 127.0), 8, axis=1)[..., None]
    return vals.transpose(0, 1, 3, 2).reshape(g * 512, n)
def pack4(w):
    words, scales = pack_weight(w, "e2m1")
    return words.reshape(words.shape[0], 128, -1), scales


def unpack4(words, scales):
    return unpack_weight(words.reshape(words.shape[0], 128, -1, 2), scales, "e2m1")


G, M, K, F, N = 4, 512, 1024, 512, 1024


def setup_inputs():
    s = mx_kscale(G * K).reshape(G, K)
    t = mx_kscale(G * F).reshape(G, F)
    re = np.random.standard_normal((G, M, K)) * s[:, None, :]
    im = np.random.standard_normal((G, M, K)) * s[:, None, :]
    v = np.random.standard_normal((G, K, F)) / np.sqrt(K) / s[:, :, None] * t[:, None, :]
    u = np.random.standard_normal((G, F, N)) / np.sqrt(F) / t[:, :, None]
    v_words, v_scales = pack4(v.reshape(G * K, F))
    u_words, u_scales = pack4(u.reshape(G * F, N))
    return {"re": bf(re),
            "im": bf(im),
            "phase": bf(np.random.uniform(0.1, 1.5, (G, F))),
            "v_words": v_words, "v_scales": v_scales,
            "u_words": u_words, "u_scales": u_scales}


def reference(re, im, phase, v_words, v_scales, u_words, u_scales):
    v = unpack4(v_words, v_scales).reshape(G, K, F)
    u = unpack4(u_words, u_scales).reshape(G, F, N)
    a = mxq(f64(re), 2, "e4m3") @ v
    b = mxq(f64(im), 2, "e4m3") @ v
    theta = f64(phase)[:, None, :]
    z = a * np.cos(theta) + b * np.sin(theta)
    return mxq(z, 2, "e4m3") @ u

@@ -1,0 +1,435 @@
+from contextlib import ExitStack
+import math
+
+import concourse.mybir as mybir
+from concourse.masks import make_identity
+
+G, M, K, F, N = 4, 512, 1024, 512, 1024
+FLOPS = 2 * G * (2 * M * K * F + M * F * N)
+
+F32 = mybir.dt.float32
+BF16 = mybir.dt.bfloat16
+U32 = mybir.dt.uint32
+I32 = mybir.dt.int32
+U8 = mybir.dt.uint8
+FP8X4 = mybir.dt.float8_e4m3fn_x4
+FP4X4 = mybir.dt.float4_e2m1fn_x4
+ALU = mybir.AluOpType
+ACT = mybir.ActivationFunctionType
+P = 128
+
+
+def tile_split_real_schrodinger_step_s14_kernel(tc, re, im, phase, v_words, v_scales, u_words, u_scales, out):
+    nc = tc.nc
+    with ExitStack() as ctx:
+        keep = ctx.enter_context(tc.tile_pool(name="keep", bufs=1))
+        work = ctx.enter_context(tc.tile_pool(name="work", bufs=3))
+        psum = ctx.enter_context(tc.psum_pool(name="psum", bufs=8))
+        ctx.enter_context(tc.manual_schedule())
+
+        x = {}
+        for c in range(G):
+            for part in range(2):
+                xt = keep.tile([P, 4, K], BF16, name="x%d_%d" % (c, part))
+                x[c, part] = xt
+        vraw = []
+        vperm = []
+        u = []
+        for c in range(G):
+            t0 = keep.tile([P, 2, 1024], U8, name="vraw%d" % c, align_bytes=256)
+            t1 = keep.tile([P, 2, 4, 256], U8, name="vperm%d" % c, align_bytes=256)
+            t2 = keep.tile([P, 2048], U8, name="u%d" % c, align_bytes=256)
+            vraw.append(t0)
+            vperm.append(t1)
+            u.append(t2)
+        sraw = keep.tile([P, 8, 512], U8, name="sraw", align_bytes=256)
+        sperm = []
+        for c in range(G):
+            t3 = keep.tile([P, 2, 4, 128], U8, name="sperm%d" % c, align_bytes=256)
+            sperm.append(t3)
+        us = keep.tile([P, 4, 1024], U8, name="us", align_bytes=256)
+        ident = keep.tile([P, P], F32, name="ident")
+        ph = keep.tile([P, G, 4], BF16, name="ph")
+        turns = keep.tile([P, G * 4], I32, name="turns")
+        arg = keep.tile([P, 2, G * 4], F32, name="arg")
+        high = keep.tile([P, 2, G * 4], F32, name="high")
+        low = keep.tile([P, 2, G * 4], F32, name="low")
+        sc = keep.tile([P, 2, G * 4], F32, name="sc")
+        dummy = keep.tile([P, 1], F32, name="dummy")
+
+        src = (re, im)
+
+        def load_rows(c, part, i0, i1):
+            nc.sync.dma_start(out=x[c, part][:, i0:i1, :], in_=src[part][c].rearrange("(p i) k -> p i k", i=4)[:, i0:i1, :])
+
+        def load_all(c, part):
+            load_rows(c, part, 0, 4)
+
+        def load_v(c):
+            nc.sync.dma_start(out=vraw[c][:].bitcast(I32), in_=v_words[2 * c : 2 * c + 2].bitcast(I32).rearrange("g p b -> p g b"))
+
+        def load_u(c):
+            nc.sync.dma_start(out=u[c][:].bitcast(I32), in_=u_words[c].bitcast(I32))
+
+        nc.scalar.dma_start(out=ph[:], in_=phase.rearrange("c (p t) -> p c t", t=4))
+        nc.vector.memset(dummy[:], 0.0)
+        nc.vector.memset(sraw[:].bitcast(I32), 0)
+        nc.scalar.activation(out=dummy[:], in_=dummy[:], func=ACT.Sin)
+        make_identity(nc, ident[:])
+        nc.gpsimd.memset(us[:].bitcast(I32), 0)
+
+        load_rows(0, 0, 0, 1)
+        load_rows(0, 0, 1, 2)
+        load_rows(0, 0, 2, 4)
+        load_v(0)
+        for q in range(4):
+            nc.sync.dma_start(
+                out=sraw[:].bitcast(I32)[32 * q : 32 * q + 4, :, :],
+                in_=v_scales.bitcast(I32)[:, 4 * q : 4 * q + 4, :].rearrange("g r n -> r g n"),
+            )
+        load_rows(0, 1, 0, 2)
+        load_rows(0, 1, 2, 4)
+        load_all(1, 0)
+        load_v(1)
+        load_all(1, 1)
+        load_u(0)
+        for q in range(4):
+            nc.sync.dma_start(
+                out=us[:].bitcast(I32)[32 * q : 32 * q + 4, :, :],
+                in_=u_scales.bitcast(I32)[:, 4 * q : 4 * q + 4, :].rearrange("c r n -> r c n"),
+            )
+        load_all(2, 0)
+        load_v(2)
+        load_all(2, 1)
+        load_u(1)
+        load_all(3, 0)
+        load_v(3)
+        load_all(3, 1)
+        load_u(2)
+        load_u(3)
+
+        phf = ph[:].rearrange("p c t -> p (c t)")
+        angle = arg[:, 0, :]
+
+        def trig_turns():
+            nc.vector.tensor_scalar(out=turns[:], in0=phf, scalar1=1.0 / (2.0 * math.pi), scalar2=None, op0=ALU.mult)
+
+        def trig_reduce():
+            nc.vector.scalar_tensor_tensor(out=angle, in0=turns[:], scalar=-2.0 * math.pi, in1=phf, op0=ALU.mult, op1=ALU.add)
+
+        def trig_wrap():
+            nc.gpsimd.tensor_scalar(out=arg[:, 1, :], in0=angle, scalar1=1.0, scalar2=0.5 * math.pi, op0=ALU.mult, op1=ALU.add)
+            nc.gpsimd.tensor_scalar(out=high[:], in0=arg[:], scalar1=math.pi, scalar2=-2.0 * math.pi, op0=ALU.is_gt, op1=ALU.mult)
+            nc.gpsimd.tensor_scalar(out=low[:], in0=arg[:], scalar1=-math.pi, scalar2=2.0 * math.pi, op0=ALU.is_lt, op1=ALU.mult)
+            nc.gpsimd.tensor_tensor(out=arg[:], in0=arg[:], in1=high[:], op=ALU.add)
+            nc.gpsimd.tensor_tensor(out=arg[:], in0=arg[:], in1=low[:], op=ALU.add)
+
+        def trig_sin():
+            nc.scalar.activation(out=sc[:], in_=arg[:], func=ACT.Sin)
+
+        def bank():
+            b = psum.tile([P, 512], F32, name="bank")
+            return b
+
+        grouped = {}
+        codes = {}
+        scales = {}
+
+        def new_unit(c, part):
+            gt = work.tile([P, 2, 2048], BF16, name="grouped", bufs=4, align_bytes=256)
+            ct = work.tile([P, 2, 512], U32, name="codes", bufs=4, align_bytes=256)
+            st = work.tile([P, 2, 512], U8, name="scales", bufs=4, align_bytes=256)
+            grouped[c, part] = gt
+            codes[c, part] = ct
+            scales[c, part] = st
+
+        sorted_words = {}
+
+        def sort_words(c, part, i):
+            w = work.tile([P, 512], F32, name="sorted_words", bufs=4)
+            sorted_words[c, part, i] = w
+            nc.vector.tensor_copy(
+                out=w[:].rearrange("p (g u r) -> p g u r", g=2, u=2),
+                in_=x[c, part][:].bitcast(F32)[:, i, :].rearrange("p (g r u) -> p g u r", g=2, u=2),
+            )
+
+        banks = {}
+
+        def turn(c, part, i):
+            words = x[c, part][:].bitcast(F32)
+            b = bank()
+            banks["T", c, part, i] = b
+            bv = b[:].rearrange("p (g u r) -> p g u r", g=2, u=2)
+            for g in range(2):
+                for e in range(2):
+                    if (c, part, i) in sorted_words:
+                        w0 = 256 * g + 128 * e
+                        source = sorted_words[c, part, i][:, w0 : w0 + 128]
+                    else:
+                        source = words[:, i, 256 * g + e : 256 * (g + 1) : 2]
+                    nc.tensor.transpose(bv[:, g, e, :], source, ident[:])
+
+        def copy_out(dst, s, on_vector):
+            if on_vector:
+                nc.vector.tensor_copy(out=dst, in_=s)
+            else:
+                nc.scalar.copy(out=dst, in_=s)
+
+        def turn_out(c, part, i, on_vector):
+            if (c, part) not in grouped:
+                new_unit(c, part)
+            dst = grouped[c, part][:].bitcast(F32).rearrange("p g (n u) -> p g n u", u=2)[:, :, 128 * i : 128 * (i + 1), :]
+            copy_out(dst, banks["T", c, part, i][:].rearrange("p (g u r) -> p g r u", g=2, u=2), on_vector)
+
+        def quantize(c, part, g, i0=0, i1=4):
+            cols = slice(128 * i0, 128 * i1)
+            nc.vector.quantize_mx(
+                out=codes[c, part][:, g, cols].bitcast(FP8X4), scales=scales[c, part][:, g, cols],
+                in_=grouped[c, part][:, g, 512 * i0 : 512 * i1],
+            )
+
+        def permute_codes(c):
+            for g in range(2):
+                permute_group(c, g)
+
+        def permute_group(c, g):
+            if True:
+                nc.vector.tensor_copy(
+                    out=vperm[c][:, g, :, :].rearrange("p t (m b) -> p t m b", b=2),
+                    in_=vraw[c][:, g, :].rearrange("p (m t b) -> p t m b", t=4, b=2),
+                )
+
+        def permute_scales(c):
+            nc.vector.tensor_copy(out=sperm[c][:], in_=sraw[:, 2 * c : 2 * c + 2, :].rearrange("p g (m t) -> p g t m", t=4))
+
+        def project(c, part, t):
+            b = bank()
+            for g in range(2):
+                nc.tensor.matmul_mx(
+                    out=b[:],
+                    lhsT=vperm[c][:, g, t, :].bitcast(FP4X4),
+                    lhsT_scale=sperm[c][:, g, t, :],
+                    rhs=codes[c, part][:, g, :].bitcast(FP8X4),
+                    rhs_scale=scales[c, part][:, g, :],
+                    start=(g == 0),
+                    stop=(g == 1),
+                )
+            return b
+
+        acos = {}
+        zrows = {}
+        zgroup = {}
+        zcodes = {}
+        zscales = {}
+
+        def real_out(c, t):
+            a = work.tile([P, 512], F32, name="acos", bufs=6)
+            acos[c, t] = a
+            nc.scalar.activation(out=a[:], in_=banks["A", c, t][:], func=ACT.Copy, scale=sc[:, 1, 4 * c + t : 4 * c + t + 1])
+
+        def new_z(c):
+            z0 = work.tile([P, 4, 512], BF16, name="zrows", bufs=2)
+            z1 = work.tile([P, 512, 4], BF16, name="zgroup", bufs=2, align_bytes=256)
+            z2 = work.tile([P, 512], U32, name="zcodes", bufs=2, align_bytes=256)
+            z3 = work.tile([P, 512], U8, name="zscales", bufs=2, align_bytes=256)
+            zrows[c] = z0
+            zgroup[c] = z1
+            zcodes[c] = z2
+            zscales[c] = z3
+
+        def add_imag(c, t, cols, b):
+            if c not in zrows:
+                new_z(c)
+            nc.vector.scalar_tensor_tensor(
+                out=zrows[c][:, t, cols], in0=b, scalar=sc[:, 0, 4 * c + t : 4 * c + t + 1], in1=acos[c, t][:, cols],
+                op0=ALU.mult, op1=ALU.add,
+            )
+
+        def imag_half(c, h, j):
+            b = bank()
+            banks["B", c, 2 * h + j] = b
+            for k in range(2):
+                t = 2 * j + k
+                for r in range(2):
+                    cols = slice(256 * h + 128 * r, 256 * h + 128 * (r + 1))
+                    for g in range(2):
+                        nc.tensor.matmul_mx(
+                            out=b[:, 256 * k + 128 * r : 256 * k + 128 * (r + 1)],
+                            lhsT=vperm[c][:, g, t, :].bitcast(FP4X4),
+                            lhsT_scale=sperm[c][:, g, t, :],
+                            rhs=codes[c, 1][:, g, cols].bitcast(FP8X4),
+                            rhs_scale=scales[c, 1][:, g, cols],
+                            start=(g == 0),
+                            stop=(g == 1),
+                        )
+
+        def add_imag_half(c, h, j):
+            b = banks["B", c, 2 * h + j]
+            for k in range(2):
+                add_imag(c, 2 * j + k, slice(256 * h, 256 * (h + 1)), b[:, 256 * k : 256 * (k + 1)])
+
+        def project_row(c, i):
+            b = bank()
+            cols = slice(128 * i, 128 * (i + 1))
+            for t in range(4):
+                for g in range(2):
+                    nc.tensor.matmul_mx(
+                        out=b[:, 128 * t : 128 * (t + 1)],
+                        lhsT=vperm[c][:, g, t, :].bitcast(FP4X4),
+                        lhsT_scale=sperm[c][:, g, t, :],
+                        rhs=codes[c, 1][:, g, cols].bitcast(FP8X4),
+                        rhs_scale=scales[c, 1][:, g, cols],
+                        start=(g == 0),
+                        stop=(g == 1),
+                    )
+            return b
+
+        def add_imag_row(c, i, b):
+            for t in range(4):
+                add_imag(c, t, slice(128 * i, 128 * (i + 1)), b[:, 128 * t : 128 * (t + 1)])
+
+        def interleave(c, i, j, on_scalar=False):
+            cols = slice(128 * i, 128 * j)
+            dst = zgroup[c][:, cols, :]
+            source = zrows[c][:, :, cols].rearrange("p t n -> p n t")
+            if on_scalar:
+                nc.scalar.copy(out=dst, in_=source)
+            else:
+                nc.vector.tensor_copy(out=dst, in_=source)
+
+        def quantize_z(c, i, j):
+            cols = slice(128 * i, 128 * j)
+            nc.vector.quantize_mx(
+                out=zcodes[c][:, cols].bitcast(FP8X4), scales=zscales[c][:, cols],
+                in_=zgroup[c][:, cols, :].rearrange("p n t -> p (n t)"),
+            )
+
+        out_rows = {}
+
+        def expand(c, i, n):
+            cols = slice(128 * i, 128 * (i + 1))
+            b = bank()
+            banks["O", c, i, n] = b
+            nc.tensor.matmul_mx(
+                out=b[:],
+                lhsT=zcodes[c][:, cols].bitcast(FP8X4),
+                lhsT_scale=zscales[c][:, cols],
+                rhs=u[c][:, 1024 * n : 1024 * (n + 1)].bitcast(FP4X4),
+                rhs_scale=us[:, c, 512 * n : 512 * (n + 1)],
+                start=True,
+                stop=True,
+            )
+
+        def expand_out(c, i, n, on_vector):
+            second = (c, i) in out_rows
+            if not second:
+                o = work.tile([P, 1024], F32, name="orow", bufs=8)
+                out_rows[c, i] = o
+            cols = slice(512 * n, 512 * (n + 1))
+            copy_out(out_rows[c, i][:, cols], banks["O", c, i, n][:], on_vector)
+            if c == 3 and i == 3:
+                nc.sync.dma_start(out=out[c].rearrange("(p i) n -> p i n", i=4)[:, i, cols], in_=out_rows[c, i][:, cols])
+            elif second:
+                nc.sync.dma_start(out=out[c].rearrange("(p i) n -> p i n", i=4)[:, i, :], in_=out_rows[c, i][:])
+
+        def turn_run(c, part, on_vector):
+            for i in range(4):
+                turn(c, part, i)
+                turn_out(c, part, i, i in on_vector)
+
+        def real_run(c):
+            for t in range(4):
+                banks["A", c, t] = project(c, 0, t)
+                real_out(c, t)
+
+        def imag_run(c):
+            for t in range(4):
+                banks["B", c, t] = project(c, 1, t)
+                add_imag(c, t, slice(0, 512), banks["B", c, t][:])
+
+        def expand_row(c, i, on_vector):
+            for n in range(2):
+                expand(c, i, n)
+                expand_out(c, i, n, n in on_vector)
+
+        def quantize_rows(c):
+            interleave(c, 0, 2)
+            interleave(c, 2, 4)
+            quantize_z(c, 0, 2)
+            quantize_z(c, 2, 4)
+
+        def quantize_all(c, part):
+            nc.vector.quantize_mx(
+                out=codes[c, part][:].rearrange("p g n -> p (g n)").bitcast(FP8X4),
+                scales=scales[c, part][:].rearrange("p g n -> p (g n)"),
+                in_=grouped[c, part][:].rearrange("p g n -> p (g n)"),
+            )
+
+        for i in range(4):
+            sort_words(0, 0, i)
+            turn(0, 0, i)
+            turn_out(0, 0, i, False)
+            if i == 1:
+                trig_turns()
+            if i == 2:
+                trig_reduce()
+        trig_wrap()
+        permute_group(0, 0)
+        quantize(0, 0, 0, 0, 2)
+        quantize(0, 0, 1, 0, 2)
+        permute_group(0, 1)
+        quantize(0, 0, 0, 2, 4)
+        quantize(0, 0, 1, 2, 4)
+        permute_scales(0)
+        turn_run(0, 1, ())
+        trig_sin()
+        permute_scales(1)
+        real_run(0)
+        quantize_all(0, 1)
+        permute_group(1, 0)
+        permute_group(1, 1)
+        turn_run(1, 0, (1, 3))
+        imag_run(0)
+        quantize_all(1, 0)
+
+        for c in range(3):
+            turn_run(c + 1, 1, ())
+            if c < 2:
+                permute_group(c + 2, 0)
+            quantize_rows(c)
+            quantize_all(c + 1, 1)
+            real_run(c + 1)
+            if c < 2:
+                permute_group(c + 2, 1)
+                permute_scales(c + 2)
+                turn_run(c + 2, 0, (3,))
+                expand_row(c, 0, ())
+                expand_row(c, 1, (0,))
+                expand_row(c, 2, (0,))
+                expand_row(c, 3, ())
+                quantize_all(c + 2, 0)
+                imag_run(c + 1)
+
+        expand_row(2, 0, (0,))
+        expand_row(2, 1, (0,))
+        for j in range(2):
+            imag_half(3, 0, j)
+            add_imag_half(3, 0, j)
+        expand_row(2, 2, ())
+        interleave(3, 0, 1)
+        interleave(3, 1, 2)
+        quantize_z(3, 0, 1)
+        b2 = project_row(3, 2)
+        add_imag_row(3, 2, b2)
+        quantize_z(3, 1, 2)
+        expand_row(2, 3, ())
+        b3 = project_row(3, 3)
+        interleave(3, 2, 3)
+        add_imag_row(3, 3, b3)
+        quantize_z(3, 2, 3)
+        expand_row(3, 0, ())
+        interleave(3, 3, 4)
+        expand_row(3, 1, ())
+        quantize_z(3, 3, 4)
+        expand_row(3, 2, (1,))
+        expand_row(3, 3, (1,))

@@ -10,6 +10,7 @@ FLOPS = 2 * G * (2 * M * K * F + M * F * N)
 F32 = mybir.dt.float32
 BF16 = mybir.dt.bfloat16
 U32 = mybir.dt.uint32
+U16 = mybir.dt.uint16
 I32 = mybir.dt.int32
 U8 = mybir.dt.uint8
 FP8X4 = mybir.dt.float8_e4m3fn_x4
@@ -17,419 +18,311 @@ FP4X4 = mybir.dt.float4_e2m1fn_x4
 ALU = mybir.AluOpType
 ACT = mybir.ActivationFunctionType
 P = 128
+UNITS = 2 * G
+BANKS = 8
 
 
 def tile_split_real_schrodinger_step_s14_kernel(tc, re, im, phase, v_words, v_scales, u_words, u_scales, out):
     nc = tc.nc
     with ExitStack() as ctx:
         keep = ctx.enter_context(tc.tile_pool(name="keep", bufs=1))
-        work = ctx.enter_context(tc.tile_pool(name="work", bufs=3))
-        psum = ctx.enter_context(tc.psum_pool(name="psum", bufs=8))
+        work = ctx.enter_context(tc.tile_pool(name="work", bufs=2))
+        psum = ctx.enter_context(tc.psum_pool(name="psum", bufs=1))
         ctx.enter_context(tc.manual_schedule())
 
-        x = {}
-        for c in range(G):
-            for part in range(2):
-                xt = keep.tile([P, 4, K], BF16, name="x%d_%d" % (c, part))
-                x[c, part] = xt
-        vraw = []
-        vperm = []
-        u = []
-        for c in range(G):
-            t0 = keep.tile([P, 2, 1024], U8, name="vraw%d" % c, align_bytes=256)
-            t1 = keep.tile([P, 2, 4, 256], U8, name="vperm%d" % c, align_bytes=256)
-            t2 = keep.tile([P, 2048], U8, name="u%d" % c, align_bytes=256)
-            vraw.append(t0)
-            vperm.append(t1)
-            u.append(t2)
-        sraw = keep.tile([P, 8, 512], U8, name="sraw", align_bytes=256)
-        sperm = []
-        for c in range(G):
-            t3 = keep.tile([P, 2, 4, 128], U8, name="sperm%d" % c, align_bytes=256)
-            sperm.append(t3)
-        us = keep.tile([P, 4, 1024], U8, name="us", align_bytes=256)
+        v_raw = [keep.tile([P, 2, 1024], U8, name="v_raw%d" % c, align_bytes=256) for c in range(G)]
+        v_dealt = [keep.tile([P, 2, 4, 256], U8, name="v_dealt%d" % c, align_bytes=256) for c in range(G)]
+        vs_raw = [keep.tile([P, 2, 512], U8, name="vs_raw0", align_bytes=256), keep.tile([P, 6, 512], U8, name="vs_raw1", align_bytes=256)]
+        vs_dealt = [keep.tile([P, 2, 4, 128], U8, name="vs_dealt%d" % c, align_bytes=256) for c in range(G)]
+        u_codes = [keep.tile([P, 2048], U8, name="u_codes%d" % c, align_bytes=256) for c in range(G)]
+        u_plane = keep.tile([P, G, 1024], U8, name="u_plane", align_bytes=256)
         ident = keep.tile([P, P], F32, name="ident")
-        ph = keep.tile([P, G, 4], BF16, name="ph")
-        turns = keep.tile([P, G * 4], I32, name="turns")
-        arg = keep.tile([P, 2, G * 4], F32, name="arg")
-        high = keep.tile([P, 2, G * 4], F32, name="high")
-        low = keep.tile([P, 2, G * 4], F32, name="low")
-        sc = keep.tile([P, 2, G * 4], F32, name="sc")
-        dummy = keep.tile([P, 1], F32, name="dummy")
+        theta = keep.tile([P, G, 4], BF16, name="theta")
+        turns = keep.tile([P, 2, 4 * G], F32, name="turns")
+        whole = keep.tile([P, 2, 4 * G], I32, name="whole")
+        rest = keep.tile([P, 2, 4 * G], F32, name="rest")
+        flipped = keep.tile([P, 2, 4 * G], F32, name="flipped")
+        wrapped = keep.tile([P, 2, 4 * G], F32, name="wrapped")
+        trig = keep.tile([P, 2, 4 * G], F32, name="trig")
 
-        src = (re, im)
+        words = {}
 
-        def load_rows(c, part, i0, i1):
-            nc.sync.dma_start(out=x[c, part][:, i0:i1, :], in_=src[part][c].rearrange("(p i) k -> p i k", i=4)[:, i0:i1, :])
+        def load_x(u, part, j0, j1):
+            c, h = divmod(u, 2)
+            xt = keep.tile([P, j1 - j0, K], BF16, name="x%d_%d_%d" % (u, part, j0))
+            rows = (re, im)[part][c].rearrange("(p i) k -> p i k", i=4)
+            nc.sync.dma_start(out=xt[:], in_=rows[:, 2 * h + j0 : 2 * h + j1, :])
+            for j in range(j0, j1):
+                words[u, 2 * part + j] = xt[:].bitcast(F32)[:, j - j0, :]
 
-        def load_all(c, part):
-            load_rows(c, part, 0, 4)
+        def load_unit(u):
+            load_x(u, 0, 0, 2)
+            load_x(u, 1, 0, 2)
 
         def load_v(c):
-            nc.sync.dma_start(out=vraw[c][:].bitcast(I32), in_=v_words[2 * c : 2 * c + 2].bitcast(I32).rearrange("g p b -> p g b"))
+            nc.sync.dma_start(out=v_raw[c][:].bitcast(I32), in_=v_words[2 * c : 2 * c + 2].bitcast(I32).rearrange("g p b -> p g b"))
 
         def load_u(c):
-            nc.sync.dma_start(out=u[c][:].bitcast(I32), in_=u_words[c].bitcast(I32))
+            nc.sync.dma_start(out=u_codes[c][:].bitcast(I32), in_=u_words[c].bitcast(I32))
 
-        nc.scalar.dma_start(out=ph[:], in_=phase.rearrange("c (p t) -> p c t", t=4))
-        nc.vector.memset(dummy[:], 0.0)
-        nc.vector.memset(sraw[:].bitcast(I32), 0)
-        nc.scalar.activation(out=dummy[:], in_=dummy[:], func=ACT.Sin)
+        def load_plane(plane, rows):
+            for q in range(4):
+                nc.sync.dma_start(
+                    out=plane[:].bitcast(I32)[32 * q : 32 * q + 4, :, :],
+                    in_=rows.bitcast(I32)[:, 4 * q : 4 * q + 4, :].rearrange("g r n -> r g n"),
+                )
+
+        nc.scalar.dma_start(out=theta[:], in_=phase.rearrange("c (p t) -> p c t", t=4))
+        nc.vector.memset(vs_raw[0][:].bitcast(I32), 0)
+        nc.vector.memset(vs_raw[1][:].bitcast(I32), 0)
         make_identity(nc, ident[:])
-        nc.gpsimd.memset(us[:].bitcast(I32), 0)
+        nc.gpsimd.memset(u_plane[:].bitcast(I32), 0)
 
-        load_rows(0, 0, 0, 1)
-        load_rows(0, 0, 1, 2)
-        load_rows(0, 0, 2, 4)
+        load_x(0, 0, 0, 1)
+        load_x(0, 0, 1, 2)
+        load_x(0, 1, 0, 1)
         load_v(0)
-        for q in range(4):
-            nc.sync.dma_start(
-                out=sraw[:].bitcast(I32)[32 * q : 32 * q + 4, :, :],
-                in_=v_scales.bitcast(I32)[:, 4 * q : 4 * q + 4, :].rearrange("g r n -> r g n"),
-            )
-        load_rows(0, 1, 0, 2)
-        load_rows(0, 1, 2, 4)
-        load_all(1, 0)
+        load_x(0, 1, 1, 2)
+        load_plane(vs_raw[0], v_scales[0:2])
+        load_unit(1)
         load_v(1)
-        load_all(1, 1)
+        load_unit(2)
+        load_plane(vs_raw[1], v_scales[2:8])
         load_u(0)
-        for q in range(4):
-            nc.sync.dma_start(
-                out=us[:].bitcast(I32)[32 * q : 32 * q + 4, :, :],
-                in_=u_scales.bitcast(I32)[:, 4 * q : 4 * q + 4, :].rearrange("c r n -> r c n"),
-            )
-        load_all(2, 0)
+        load_plane(u_plane, u_scales)
+        load_unit(3)
+        load_unit(4)
         load_v(2)
-        load_all(2, 1)
         load_u(1)
-        load_all(3, 0)
+        load_unit(5)
+        load_unit(6)
         load_v(3)
-        load_all(3, 1)
         load_u(2)
+        load_unit(7)
         load_u(3)
 
-        phf = ph[:].rearrange("p c t -> p (c t)")
-        angle = arg[:, 0, :]
+        theta_flat = theta[:].rearrange("p c t -> p (c t)")
 
         def trig_turns():
-            nc.vector.tensor_scalar(out=turns[:], in0=phf, scalar1=1.0 / (2.0 * math.pi), scalar2=None, op0=ALU.mult)
+            for s in range(2):
+                nc.vector.tensor_scalar(
+                    out=turns[:, s, :], in0=theta_flat, scalar1=0.5 / math.pi, scalar2=0.25 * s, op0=ALU.mult, op1=ALU.add
+                )
 
-        def trig_reduce():
-            nc.vector.scalar_tensor_tensor(out=angle, in0=turns[:], scalar=-2.0 * math.pi, in1=phf, op0=ALU.mult, op1=ALU.add)
+        def trig_whole():
+            nc.vector.tensor_copy(out=whole[:], in_=turns[:])
 
-        def trig_wrap():
-            nc.gpsimd.tensor_scalar(out=arg[:, 1, :], in0=angle, scalar1=1.0, scalar2=0.5 * math.pi, op0=ALU.mult, op1=ALU.add)
-            nc.gpsimd.tensor_scalar(out=high[:], in0=arg[:], scalar1=math.pi, scalar2=-2.0 * math.pi, op0=ALU.is_gt, op1=ALU.mult)
-            nc.gpsimd.tensor_scalar(out=low[:], in0=arg[:], scalar1=-math.pi, scalar2=2.0 * math.pi, op0=ALU.is_lt, op1=ALU.mult)
-            nc.gpsimd.tensor_tensor(out=arg[:], in0=arg[:], in1=high[:], op=ALU.add)
-            nc.gpsimd.tensor_tensor(out=arg[:], in0=arg[:], in1=low[:], op=ALU.add)
+        def trig_rest():
+            nc.vector.scalar_tensor_tensor(out=rest[:], in0=whole[:], scalar=-1.0, in1=turns[:], op0=ALU.mult, op1=ALU.add)
+
+        def trig_wrap(dst, src):
+            nc.vector.scalar_tensor_tensor(out=dst[:], in0=src[:], scalar=0.5, in1=src[:], op0=ALU.is_gt, op1=ALU.subtract)
 
         def trig_sin():
-            nc.scalar.activation(out=sc[:], in_=arg[:], func=ACT.Sin)
+            nc.scalar.activation(out=trig[:], in_=wrapped[:], func=ACT.Sin, scale=2.0 * math.pi)
 
-        def bank():
-            b = psum.tile([P, 512], F32, name="bank")
+        banks = {}
+        taken = []
+
+        def new_bank(key):
+            b = psum.tile([P, 512], F32, name="bank%d" % (len(taken) % BANKS))
+            taken.append(key)
+            banks[key] = b
             return b
+
+        def copy_on(engine, dst, src):
+            if engine == "vector":
+                nc.vector.tensor_copy(out=dst, in_=src)
+            else:
+                nc.scalar.copy(out=dst, in_=src)
+
+        sorted_words = {}
+
+        def sort_words(u, q):
+            w = work.tile([P, 512], F32, name="sorted_words", bufs=8)
+            sorted_words[u, q] = w
+            nc.vector.tensor_copy(
+                out=w[:].rearrange("p (g e r) -> p g e r", g=2, e=2),
+                in_=words[u, q].rearrange("p (g r e) -> p g e r", g=2, e=2),
+            )
+
+        def turn(u, q):
+            b = new_bank(("T", u, q))
+            for g in range(2):
+                for e in range(2):
+                    w0 = 256 * g + 128 * e
+                    if (u, q) in sorted_words:
+                        source = sorted_words[u, q][:, w0 : w0 + 128]
+                    else:
+                        source = words[u, q][:, 256 * g + e : 256 * (g + 1) : 2]
+                    nc.tensor.transpose(b[:, w0 : w0 + 128], source, ident[:])
 
         grouped = {}
         codes = {}
         scales = {}
 
-        def new_unit(c, part):
-            gt = work.tile([P, 2, 2048], BF16, name="grouped", bufs=4, align_bytes=256)
-            ct = work.tile([P, 2, 512], U32, name="codes", bufs=4, align_bytes=256)
-            st = work.tile([P, 2, 512], U8, name="scales", bufs=4, align_bytes=256)
-            grouped[c, part] = gt
-            codes[c, part] = ct
-            scales[c, part] = st
+        def turn_out(u, q, engine):
+            if u not in grouped:
+                grouped[u] = work.tile([P, 2, 2048], BF16, name="grouped", bufs=2, align_bytes=256)
+                codes[u] = work.tile([P, 2, 512], U32, name="codes", bufs=3, align_bytes=256)
+                scales[u] = work.tile([P, 2, 512], U8, name="scales", bufs=3, align_bytes=256)
+            dst = grouped[u][:].bitcast(F32).rearrange("p g (n e) -> p g n e", e=2)[:, :, 128 * q : 128 * (q + 1), :]
+            copy_on(engine, dst, banks["T", u, q][:].rearrange("p (g e r) -> p g r e", g=2, e=2))
 
-        sorted_words = {}
+        def quantize_x(u, g):
+            nc.vector.quantize_mx(out=codes[u][:, g, :].bitcast(FP8X4), scales=scales[u][:, g, :], in_=grouped[u][:, g, :])
 
-        def sort_words(c, part, i):
-            w = work.tile([P, 512], F32, name="sorted_words", bufs=4)
-            sorted_words[c, part, i] = w
+        def deal_codes(c, g):
             nc.vector.tensor_copy(
-                out=w[:].rearrange("p (g u r) -> p g u r", g=2, u=2),
-                in_=x[c, part][:].bitcast(F32)[:, i, :].rearrange("p (g r u) -> p g u r", g=2, u=2),
+                out=v_dealt[c][:].bitcast(U16)[:, g, :, :],
+                in_=v_raw[c][:].bitcast(U16)[:, g, :].rearrange("p (m t) -> p t m", t=4),
             )
 
-        banks = {}
+        def deal_scales(c, g):
+            raw = vs_raw[0][:, g, :] if c == 0 else vs_raw[1][:, 2 * (c - 1) + g, :]
+            nc.vector.tensor_copy(out=vs_dealt[c][:, g, :, :], in_=raw.rearrange("p (m t) -> p t m", t=4))
 
-        def turn(c, part, i):
-            words = x[c, part][:].bitcast(F32)
-            b = bank()
-            banks["T", c, part, i] = b
-            bv = b[:].rearrange("p (g u r) -> p g u r", g=2, u=2)
-            for g in range(2):
-                for e in range(2):
-                    if (c, part, i) in sorted_words:
-                        w0 = 256 * g + 128 * e
-                        source = sorted_words[c, part, i][:, w0 : w0 + 128]
-                    else:
-                        source = words[:, i, 256 * g + e : 256 * (g + 1) : 2]
-                    nc.tensor.transpose(bv[:, g, e, :], source, ident[:])
-
-        def copy_out(dst, s, on_vector):
-            if on_vector:
-                nc.vector.tensor_copy(out=dst, in_=s)
-            else:
-                nc.scalar.copy(out=dst, in_=s)
-
-        def turn_out(c, part, i, on_vector):
-            if (c, part) not in grouped:
-                new_unit(c, part)
-            dst = grouped[c, part][:].bitcast(F32).rearrange("p g (n u) -> p g n u", u=2)[:, :, 128 * i : 128 * (i + 1), :]
-            copy_out(dst, banks["T", c, part, i][:].rearrange("p (g u r) -> p g r u", g=2, u=2), on_vector)
-
-        def quantize(c, part, g, i0=0, i1=4):
-            cols = slice(128 * i0, 128 * i1)
-            nc.vector.quantize_mx(
-                out=codes[c, part][:, g, cols].bitcast(FP8X4), scales=scales[c, part][:, g, cols],
-                in_=grouped[c, part][:, g, 512 * i0 : 512 * i1],
-            )
-
-        def permute_codes(c):
-            for g in range(2):
-                permute_group(c, g)
-
-        def permute_group(c, g):
-            if True:
-                nc.vector.tensor_copy(
-                    out=vperm[c][:, g, :, :].rearrange("p t (m b) -> p t m b", b=2),
-                    in_=vraw[c][:, g, :].rearrange("p (m t b) -> p t m b", t=4, b=2),
-                )
-
-        def permute_scales(c):
-            nc.vector.tensor_copy(out=sperm[c][:], in_=sraw[:, 2 * c : 2 * c + 2, :].rearrange("p g (m t) -> p g t m", t=4))
-
-        def project(c, part, t):
-            b = bank()
+        def project(u, t):
+            c = u // 2
+            b = new_bank(("AB", u, t))
             for g in range(2):
                 nc.tensor.matmul_mx(
                     out=b[:],
-                    lhsT=vperm[c][:, g, t, :].bitcast(FP4X4),
-                    lhsT_scale=sperm[c][:, g, t, :],
-                    rhs=codes[c, part][:, g, :].bitcast(FP8X4),
-                    rhs_scale=scales[c, part][:, g, :],
+                    lhsT=v_dealt[c][:, g, t, :].bitcast(FP4X4),
+                    lhsT_scale=vs_dealt[c][:, g, t, :],
+                    rhs=codes[u][:, g, :].bitcast(FP8X4),
+                    rhs_scale=scales[u][:, g, :],
                     start=(g == 0),
                     stop=(g == 1),
                 )
-            return b
 
-        acos = {}
-        zrows = {}
-        zgroup = {}
-        zcodes = {}
-        zscales = {}
+        a_cos = {}
+        z_rows = {}
+        z_grouped = {}
+        z_codes = {}
+        z_scales = {}
 
-        def real_out(c, t):
-            a = work.tile([P, 512], F32, name="acos", bufs=6)
-            acos[c, t] = a
-            nc.scalar.activation(out=a[:], in_=banks["A", c, t][:], func=ACT.Copy, scale=sc[:, 1, 4 * c + t : 4 * c + t + 1])
+        def real_part(u, t):
+            a_cos[u, t] = work.tile([P, 256], F32, name="a_cos", bufs=4)
+            col = 4 * (u // 2) + t
+            nc.scalar.activation(out=a_cos[u, t][:], in_=banks["AB", u, t][:, 0:256], func=ACT.Copy, scale=trig[:, 1, col : col + 1])
 
-        def new_z(c):
-            z0 = work.tile([P, 4, 512], BF16, name="zrows", bufs=2)
-            z1 = work.tile([P, 512, 4], BF16, name="zgroup", bufs=2, align_bytes=256)
-            z2 = work.tile([P, 512], U32, name="zcodes", bufs=2, align_bytes=256)
-            z3 = work.tile([P, 512], U8, name="zscales", bufs=2, align_bytes=256)
-            zrows[c] = z0
-            zgroup[c] = z1
-            zcodes[c] = z2
-            zscales[c] = z3
-
-        def add_imag(c, t, cols, b):
-            if c not in zrows:
-                new_z(c)
+        def add_imag(u, t):
+            if u not in z_rows:
+                z_rows[u] = work.tile([P, 4, 256], BF16, name="z_rows", bufs=2)
+                z_grouped[u] = work.tile([P, 256, 4], BF16, name="z_grouped", bufs=2, align_bytes=256)
+                z_codes[u] = work.tile([P, 256], U32, name="z_codes", bufs=2, align_bytes=256)
+                z_scales[u] = work.tile([P, 256], U8, name="z_scales", bufs=2, align_bytes=256)
+            col = 4 * (u // 2) + t
             nc.vector.scalar_tensor_tensor(
-                out=zrows[c][:, t, cols], in0=b, scalar=sc[:, 0, 4 * c + t : 4 * c + t + 1], in1=acos[c, t][:, cols],
+                out=z_rows[u][:, t, :], in0=banks["AB", u, t][:, 256:512], scalar=trig[:, 0, col : col + 1], in1=a_cos[u, t][:],
                 op0=ALU.mult, op1=ALU.add,
             )
 
-        def imag_half(c, h, j):
-            b = bank()
-            banks["B", c, 2 * h + j] = b
-            for k in range(2):
-                t = 2 * j + k
-                for r in range(2):
-                    cols = slice(256 * h + 128 * r, 256 * h + 128 * (r + 1))
-                    for g in range(2):
-                        nc.tensor.matmul_mx(
-                            out=b[:, 256 * k + 128 * r : 256 * k + 128 * (r + 1)],
-                            lhsT=vperm[c][:, g, t, :].bitcast(FP4X4),
-                            lhsT_scale=sperm[c][:, g, t, :],
-                            rhs=codes[c, 1][:, g, cols].bitcast(FP8X4),
-                            rhs_scale=scales[c, 1][:, g, cols],
-                            start=(g == 0),
-                            stop=(g == 1),
-                        )
+        def interleave(u, j0, j1):
+            cols = slice(128 * j0, 128 * j1)
+            nc.vector.tensor_copy(out=z_grouped[u][:, cols, :], in_=z_rows[u][:, :, cols].rearrange("p t n -> p n t"))
 
-        def add_imag_half(c, h, j):
-            b = banks["B", c, 2 * h + j]
-            for k in range(2):
-                add_imag(c, 2 * j + k, slice(256 * h, 256 * (h + 1)), b[:, 256 * k : 256 * (k + 1)])
-
-        def project_row(c, i):
-            b = bank()
-            cols = slice(128 * i, 128 * (i + 1))
-            for t in range(4):
-                for g in range(2):
-                    nc.tensor.matmul_mx(
-                        out=b[:, 128 * t : 128 * (t + 1)],
-                        lhsT=vperm[c][:, g, t, :].bitcast(FP4X4),
-                        lhsT_scale=sperm[c][:, g, t, :],
-                        rhs=codes[c, 1][:, g, cols].bitcast(FP8X4),
-                        rhs_scale=scales[c, 1][:, g, cols],
-                        start=(g == 0),
-                        stop=(g == 1),
-                    )
-            return b
-
-        def add_imag_row(c, i, b):
-            for t in range(4):
-                add_imag(c, t, slice(128 * i, 128 * (i + 1)), b[:, 128 * t : 128 * (t + 1)])
-
-        def interleave(c, i, j, on_scalar=False):
-            cols = slice(128 * i, 128 * j)
-            dst = zgroup[c][:, cols, :]
-            source = zrows[c][:, :, cols].rearrange("p t n -> p n t")
-            if on_scalar:
-                nc.scalar.copy(out=dst, in_=source)
-            else:
-                nc.vector.tensor_copy(out=dst, in_=source)
-
-        def quantize_z(c, i, j):
-            cols = slice(128 * i, 128 * j)
+        def quantize_z(u, j0, j1):
+            cols = slice(128 * j0, 128 * j1)
             nc.vector.quantize_mx(
-                out=zcodes[c][:, cols].bitcast(FP8X4), scales=zscales[c][:, cols],
-                in_=zgroup[c][:, cols, :].rearrange("p n t -> p (n t)"),
+                out=z_codes[u][:, cols].bitcast(FP8X4), scales=z_scales[u][:, cols],
+                in_=z_grouped[u][:, cols, :].rearrange("p n t -> p (n t)"),
             )
 
-        out_rows = {}
-
-        def expand(c, i, n):
-            cols = slice(128 * i, 128 * (i + 1))
-            b = bank()
-            banks["O", c, i, n] = b
+        def expand(u, j, n):
+            c = u // 2
+            cols = slice(128 * j, 128 * (j + 1))
+            b = new_bank(("O", u, j, n))
             nc.tensor.matmul_mx(
                 out=b[:],
-                lhsT=zcodes[c][:, cols].bitcast(FP8X4),
-                lhsT_scale=zscales[c][:, cols],
-                rhs=u[c][:, 1024 * n : 1024 * (n + 1)].bitcast(FP4X4),
-                rhs_scale=us[:, c, 512 * n : 512 * (n + 1)],
+                lhsT=z_codes[u][:, cols].bitcast(FP8X4),
+                lhsT_scale=z_scales[u][:, cols],
+                rhs=u_codes[c][:, 1024 * n : 1024 * (n + 1)].bitcast(FP4X4),
+                rhs_scale=u_plane[:, c, 512 * n : 512 * (n + 1)],
                 start=True,
                 stop=True,
             )
 
-        def expand_out(c, i, n, on_vector):
-            second = (c, i) in out_rows
-            if not second:
-                o = work.tile([P, 1024], F32, name="orow", bufs=8)
-                out_rows[c, i] = o
+        out_rows = {}
+
+        def expand_out(u, j, n, engine):
+            c, h = divmod(u, 2)
+            if (u, j) not in out_rows:
+                out_rows[u, j] = work.tile([P, 1024], F32, name="out_rows", bufs=8)
             cols = slice(512 * n, 512 * (n + 1))
-            copy_out(out_rows[c, i][:, cols], banks["O", c, i, n][:], on_vector)
-            if c == 3 and i == 3:
-                nc.sync.dma_start(out=out[c].rearrange("(p i) n -> p i n", i=4)[:, i, cols], in_=out_rows[c, i][:, cols])
-            elif second:
-                nc.sync.dma_start(out=out[c].rearrange("(p i) n -> p i n", i=4)[:, i, :], in_=out_rows[c, i][:])
+            copy_on(engine, out_rows[u, j][:, cols], banks["O", u, j, n][:])
+            dst = out[c].rearrange("(p i) n -> p i n", i=4)[:, 2 * h + j, :]
+            if u == UNITS - 1 and j == 1:
+                nc.sync.dma_start(out=dst[:, cols], in_=out_rows[u, j][:, cols])
+            elif n == 1:
+                nc.sync.dma_start(out=dst, in_=out_rows[u, j][:])
 
-        def turn_run(c, part, on_vector):
-            for i in range(4):
-                turn(c, part, i)
-                turn_out(c, part, i, i in on_vector)
-
-        def real_run(c):
-            for t in range(4):
-                banks["A", c, t] = project(c, 0, t)
-                real_out(c, t)
-
-        def imag_run(c):
-            for t in range(4):
-                banks["B", c, t] = project(c, 1, t)
-                add_imag(c, t, slice(0, 512), banks["B", c, t][:])
-
-        def expand_row(c, i, on_vector):
-            for n in range(2):
-                expand(c, i, n)
-                expand_out(c, i, n, n in on_vector)
-
-        def quantize_rows(c):
-            interleave(c, 0, 2)
-            interleave(c, 2, 4)
-            quantize_z(c, 0, 2)
-            quantize_z(c, 2, 4)
-
-        def quantize_all(c, part):
-            nc.vector.quantize_mx(
-                out=codes[c, part][:].rearrange("p g n -> p (g n)").bitcast(FP8X4),
-                scales=scales[c, part][:].rearrange("p g n -> p (g n)"),
-                in_=grouped[c, part][:].rearrange("p g n -> p (g n)"),
-            )
-
-        for i in range(4):
-            sort_words(0, 0, i)
-            turn(0, 0, i)
-            turn_out(0, 0, i, False)
-            if i == 1:
-                trig_turns()
-            if i == 2:
-                trig_reduce()
-        trig_wrap()
-        permute_group(0, 0)
-        quantize(0, 0, 0, 0, 2)
-        quantize(0, 0, 1, 0, 2)
-        permute_group(0, 1)
-        quantize(0, 0, 0, 2, 4)
-        quantize(0, 0, 1, 2, 4)
-        permute_scales(0)
-        turn_run(0, 1, ())
+        trig_turns()
+        sort_words(0, 0)
+        trig_whole()
+        turn(0, 0)
+        trig_rest()
+        sort_words(0, 1)
+        trig_wrap(flipped, rest)
+        turn(0, 1)
+        trig_wrap(wrapped, flipped)
         trig_sin()
-        permute_scales(1)
-        real_run(0)
-        quantize_all(0, 1)
-        permute_group(1, 0)
-        permute_group(1, 1)
-        turn_run(1, 0, (1, 3))
-        imag_run(0)
-        quantize_all(1, 0)
+        turn_out(0, 0, "scalar")
+        sort_words(0, 2)
+        turn_out(0, 1, "scalar")
+        turn(0, 2)
+        turn_out(0, 2, "scalar")
+        deal_codes(0, 0)
+        turn(0, 3)
+        deal_codes(0, 1)
+        turn_out(0, 3, "vector")
+        deal_scales(0, 0)
+        quantize_x(0, 0)
+        deal_scales(0, 1)
+        quantize_x(0, 1)
 
-        for c in range(3):
-            turn_run(c + 1, 1, ())
-            if c < 2:
-                permute_group(c + 2, 0)
-            quantize_rows(c)
-            quantize_all(c + 1, 1)
-            real_run(c + 1)
-            if c < 2:
-                permute_group(c + 2, 1)
-                permute_scales(c + 2)
-                turn_run(c + 2, 0, (3,))
-                expand_row(c, 0, ())
-                expand_row(c, 1, (0,))
-                expand_row(c, 2, (0,))
-                expand_row(c, 3, ())
-                quantize_all(c + 2, 0)
-                imag_run(c + 1)
+        for k in range(UNITS):
+            ahead = k + 1 < UNITS
+            if ahead:
+                for q in range(4):
+                    turn(k + 1, q)
+            if k >= 2:
+                expand_out(k - 2, 1, 1, "vector")
+            if k >= 1:
+                interleave(k - 1, 0, 2)
+            if k + 2 < UNITS:
+                sort_words(k + 2, 0)
+            if k >= 1:
+                quantize_z(k - 1, 0, 2)
+            if k + 2 < UNITS:
+                sort_words(k + 2, 1)
+                c = (k + 2) // 2
+                deal_codes(c, k % 2)
+                deal_scales(c, k % 2)
+            if ahead:
+                for q in range(4):
+                    turn_out(k + 1, q, "scalar")
+            for t in range(4):
+                project(k, t)
+                real_part(k, t)
+                add_imag(k, t)
+                if ahead and t in (0, 2):
+                    quantize_x(k + 1, t // 2)
+            if k >= 1:
+                for j in range(2):
+                    for n in range(2):
+                        expand(k - 1, j, n)
+                        if (j, n) != (1, 1):
+                            expand_out(k - 1, j, n, "scalar")
 
-        expand_row(2, 0, (0,))
-        expand_row(2, 1, (0,))
+        last = UNITS - 1
+        interleave(last, 0, 1)
+        interleave(last, 1, 2)
+        quantize_z(last, 0, 1)
+        quantize_z(last, 1, 2)
+        expand_out(last - 1, 1, 1, "vector")
         for j in range(2):
-            imag_half(3, 0, j)
-            add_imag_half(3, 0, j)
-        expand_row(2, 2, ())
-        interleave(3, 0, 1)
-        interleave(3, 1, 2)
-        quantize_z(3, 0, 1)
-        b2 = project_row(3, 2)
-        add_imag_row(3, 2, b2)
-        quantize_z(3, 1, 2)
-        expand_row(2, 3, ())
-        b3 = project_row(3, 3)
-        interleave(3, 2, 3)
-        add_imag_row(3, 3, b3)
-        quantize_z(3, 2, 3)
-        expand_row(3, 0, ())
-        interleave(3, 3, 4)
-        expand_row(3, 1, ())
-        quantize_z(3, 3, 4)
-        expand_row(3, 2, (1,))
-        expand_row(3, 3, (1,))
+            for n in range(2):
+                expand(last, j, n)
+                expand_out(last, j, n, ("scalar", "vector")[n])

@@ -20,6 +20,9 @@ ACT = mybir.ActivationFunctionType
 P = 128
 UNITS = 2 * G
 BANKS = 8
+DEALS = {1: [5, 7], 2: [8, 9], 3: [10, 11], 4: [12, 13], 5: [14, 15], 6: [], 7: []}
+SORTED = {3: 3, 4: 3, 5: 3, 6: 3, 7: 3}
+ON_VECTOR = {1: 1, 2: 1, 3: 1, 4: 1, 5: 1, 6: 1, 7: 0}
 
 
 def tile_split_real_schrodinger_step_s14_kernel(tc, re, im, phase, v_words, v_scales, u_words, u_scales, out):
@@ -41,8 +44,8 @@ def tile_split_real_schrodinger_step_s14_kernel(tc, re, im, phase, v_words, v_sc
         turns = keep.tile([P, 2, 4 * G], F32, name="turns")
         whole = keep.tile([P, 2, 4 * G], I32, name="whole")
         rest = keep.tile([P, 2, 4 * G], F32, name="rest")
-        flipped = keep.tile([P, 2, 4 * G], F32, name="flipped")
-        wrapped = keep.tile([P, 2, 4 * G], F32, name="wrapped")
+        half_sine = keep.tile([P, 2, 4 * G], F32, name="half_sine")
+        squared = keep.tile([P, 2, 4 * G], F32, name="squared")
         trig = keep.tile([P, 2, 4 * G], F32, name="trig")
 
         words = {}
@@ -80,46 +83,43 @@ def tile_split_real_schrodinger_step_s14_kernel(tc, re, im, phase, v_words, v_sc
 
         load_x(0, 0, 0, 1)
         load_x(0, 0, 1, 2)
-        load_x(0, 1, 0, 1)
         load_v(0)
+        load_x(0, 1, 0, 1)
         load_x(0, 1, 1, 2)
         load_plane(vs_raw[0], v_scales[0:2])
         load_unit(1)
-        load_v(1)
         load_unit(2)
+        load_v(1)
         load_plane(vs_raw[1], v_scales[2:8])
         load_u(0)
         load_plane(u_plane, u_scales)
         load_unit(3)
-        load_unit(4)
         load_v(2)
+        load_unit(4)
         load_u(1)
+        load_v(3)
         load_unit(5)
         load_unit(6)
-        load_v(3)
         load_u(2)
         load_unit(7)
         load_u(3)
 
         theta_flat = theta[:].rearrange("p c t -> p (c t)")
 
-        def trig_turns():
-            for s in range(2):
-                nc.vector.tensor_scalar(
-                    out=turns[:, s, :], in0=theta_flat, scalar1=0.5 / math.pi, scalar2=0.25 * s, op0=ALU.mult, op1=ALU.add
-                )
-
-        def trig_whole():
-            nc.vector.tensor_copy(out=whole[:], in_=turns[:])
-
-        def trig_rest():
+        def trig_reduce():
+            for dst in (turns, whole):
+                for s in range(2):
+                    nc.vector.tensor_scalar(
+                        out=dst[:, s, :], in0=theta_flat, scalar1=0.5 / math.pi, scalar2=-0.25 * (1 - s), op0=ALU.mult, op1=ALU.add
+                    )
             nc.vector.scalar_tensor_tensor(out=rest[:], in0=whole[:], scalar=-1.0, in1=turns[:], op0=ALU.mult, op1=ALU.add)
+            nc.scalar.activation(out=half_sine[:], in_=rest[:], func=ACT.Sin, scale=math.pi)
 
-        def trig_wrap(dst, src):
-            nc.vector.scalar_tensor_tensor(out=dst[:], in0=src[:], scalar=0.5, in1=src[:], op0=ALU.is_gt, op1=ALU.subtract)
+        def trig_square():
+            nc.vector.scalar_tensor_tensor(out=squared[:], in0=half_sine[:], scalar=-2.0, in1=half_sine[:], op0=ALU.mult, op1=ALU.mult)
 
-        def trig_sin():
-            nc.scalar.activation(out=trig[:], in_=wrapped[:], func=ACT.Sin, scale=2.0 * math.pi)
+        def trig_finish():
+            nc.vector.tensor_scalar(out=trig[:], in0=squared[:], scalar1=1.0, scalar2=None, op0=ALU.add)
 
         banks = {}
         taken = []
@@ -169,8 +169,11 @@ def tile_split_real_schrodinger_step_s14_kernel(tc, re, im, phase, v_words, v_sc
             dst = grouped[u][:].bitcast(F32).rearrange("p g (n e) -> p g n e", e=2)[:, :, 128 * q : 128 * (q + 1), :]
             copy_on(engine, dst, banks["T", u, q][:].rearrange("p (g e r) -> p g r e", g=2, e=2))
 
-        def quantize_x(u, g):
-            nc.vector.quantize_mx(out=codes[u][:, g, :].bitcast(FP8X4), scales=scales[u][:, g, :], in_=grouped[u][:, g, :])
+        def quantize_x(u, g, q0=0, q1=4):
+            cols = slice(128 * q0, 128 * q1)
+            nc.vector.quantize_mx(
+                out=codes[u][:, g, cols].bitcast(FP8X4), scales=scales[u][:, g, cols], in_=grouped[u][:, g, 512 * q0 : 512 * q1]
+            )
 
         def deal_codes(c, g):
             nc.vector.tensor_copy(
@@ -258,70 +261,113 @@ def tile_split_real_schrodinger_step_s14_kernel(tc, re, im, phase, v_words, v_sc
             elif n == 1:
                 nc.sync.dma_start(out=dst, in_=out_rows[u, j][:])
 
-        trig_turns()
-        sort_words(0, 0)
-        trig_whole()
+        def deal(piece):
+            c, half = divmod(piece, 4)
+            (deal_codes, deal_scales)[half % 2](c, half // 2)
+
+        def project_out(u, t):
+            project(u, t)
+            real_part(u, t)
+
+        trig_reduce()
         turn(0, 0)
-        trig_rest()
-        sort_words(0, 1)
-        trig_wrap(flipped, rest)
         turn(0, 1)
-        trig_wrap(wrapped, flipped)
-        trig_sin()
+        deal_codes(0, 0)
+        trig_square()
+        deal_codes(0, 1)
+        trig_finish()
         turn_out(0, 0, "scalar")
-        sort_words(0, 2)
         turn_out(0, 1, "scalar")
+        quantize_x(0, 0, 0, 2)
+        quantize_x(0, 1, 0, 2)
         turn(0, 2)
         turn_out(0, 2, "scalar")
-        deal_codes(0, 0)
-        turn(0, 3)
-        deal_codes(0, 1)
-        turn_out(0, 3, "vector")
         deal_scales(0, 0)
-        quantize_x(0, 0)
+        quantize_x(0, 0, 2, 3)
+        quantize_x(0, 1, 2, 3)
+        turn(0, 3)
+        turn_out(0, 3, "scalar")
         deal_scales(0, 1)
-        quantize_x(0, 1)
+        quantize_x(0, 0, 3, 4)
+        quantize_x(0, 1, 3, 4)
+        for q in (0, 1):
+            turn(1, q)
+            turn_out(1, q, "scalar")
+        sort_words(1, 2)
+        sort_words(1, 3)
+        project_out(0, 0)
+        sort_words(2, 0)
+        sort_words(2, 1)
+        add_imag(0, 0)
+        project_out(0, 1)
+        sort_words(2, 2)
+        sort_words(2, 3)
+        add_imag(0, 1)
+        for q in (2, 3):
+            turn(1, q)
+            turn_out(1, q, "scalar")
+        deal(4)
+        deal(6)
+        project_out(0, 2)
+        quantize_x(1, 0)
+        add_imag(0, 2)
+        project_out(0, 3)
+        quantize_x(1, 1)
+        add_imag(0, 3)
 
-        for k in range(UNITS):
+        pending = []
+        for k in range(1, UNITS):
             ahead = k + 1 < UNITS
+            sorting = (0, 2, 1, 3)[: SORTED[k + 2] if k + 2 < UNITS else 0]
+            dealing = DEALS[k]
             if ahead:
-                for q in range(4):
+                for q in (0, 1):
                     turn(k + 1, q)
-            if k >= 2:
-                expand_out(k - 2, 1, 1, "vector")
-            if k >= 1:
-                interleave(k - 1, 0, 2)
-            if k + 2 < UNITS:
-                sort_words(k + 2, 0)
-            if k >= 1:
-                quantize_z(k - 1, 0, 2)
-            if k + 2 < UNITS:
-                sort_words(k + 2, 1)
-                c = (k + 2) // 2
-                deal_codes(c, k % 2)
-                deal_scales(c, k % 2)
+            for j, n in pending:
+                expand_out(k - 2, j, n, "vector")
+            interleave(k - 1, 0, 2)
+            for q in sorting[:1]:
+                sort_words(k + 2, q)
+            quantize_z(k - 1, 0, 2)
             if ahead:
-                for q in range(4):
+                for q in (0, 1):
                     turn_out(k + 1, q, "scalar")
-            for t in range(4):
-                project(k, t)
-                real_part(k, t)
-                add_imag(k, t)
-                if ahead and t in (0, 2):
-                    quantize_x(k + 1, t // 2)
-            if k >= 1:
-                for j in range(2):
-                    for n in range(2):
-                        expand(k - 1, j, n)
-                        if (j, n) != (1, 1):
-                            expand_out(k - 1, j, n, "scalar")
+            project_out(k, 0)
+            add_imag(k, 0)
+            for piece in dealing[:1]:
+                deal(piece)
+            project_out(k, 1)
+            add_imag(k, 1)
+            if ahead:
+                for q in (2, 3):
+                    turn(k + 1, q)
+                    turn_out(k + 1, q, "scalar")
+            for q in sorting[1:]:
+                sort_words(k + 2, q)
+            for piece in dealing[1:]:
+                deal(piece)
+            project_out(k, 2)
+            if ahead:
+                quantize_x(k + 1, 0)
+            add_imag(k, 2)
+            project_out(k, 3)
+            if ahead:
+                quantize_x(k + 1, 1)
+            add_imag(k, 3)
+            blocks = [(j, n) for j in range(2) for n in range(2)]
+            pending = blocks[4 - ON_VECTOR[k] :]
+            for j, n in blocks:
+                expand(k - 1, j, n)
+                if (j, n) not in pending:
+                    expand_out(k - 1, j, n, "scalar")
 
         last = UNITS - 1
         interleave(last, 0, 1)
         interleave(last, 1, 2)
         quantize_z(last, 0, 1)
         quantize_z(last, 1, 2)
-        expand_out(last - 1, 1, 1, "vector")
+        for j, n in pending:
+            expand_out(last - 1, j, n, "vector")
         for j in range(2):
             for n in range(2):
                 expand(last, j, n)

@@ -18,11 +18,9 @@ FP4X4 = mybir.dt.float4_e2m1fn_x4
 ALU = mybir.AluOpType
 ACT = mybir.ActivationFunctionType
 P = 128
-UNITS = 2 * G
+SETS = 2 * G
+LAST = G - 1
 BANKS = 8
-DEALS = {1: [5, 7], 2: [8, 9], 3: [10, 11], 4: [12, 13], 5: [14, 15], 6: [], 7: []}
-SORTED = {3: 3, 4: 3, 5: 3, 6: 3, 7: 3}
-ON_VECTOR = {1: 1, 2: 1, 3: 1, 4: 1, 5: 1, 6: 1, 7: 0}
 
 
 def tile_split_real_schrodinger_step_s14_kernel(tc, re, im, phase, v_words, v_scales, u_words, u_scales, out):
@@ -49,18 +47,27 @@ def tile_split_real_schrodinger_step_s14_kernel(tc, re, im, phase, v_words, v_sc
         trig = keep.tile([P, 2, 4 * G], F32, name="trig")
 
         words = {}
+        word_pairs = {}
 
-        def load_x(u, part, j0, j1):
-            c, h = divmod(u, 2)
-            xt = keep.tile([P, j1 - j0, K], BF16, name="x%d_%d_%d" % (u, part, j0))
-            rows = (re, im)[part][c].rearrange("(p i) k -> p i k", i=4)
-            nc.sync.dma_start(out=xt[:], in_=rows[:, 2 * h + j0 : 2 * h + j1, :])
-            for j in range(j0, j1):
-                words[u, 2 * part + j] = xt[:].bitcast(F32)[:, j - j0, :]
+        def tile_rows(s, q):
+            c = s // 2
+            if c < LAST:
+                return s % 2, q
+            return q // 2, 2 * (s % 2) + q % 2
 
-        def load_unit(u):
-            load_x(u, 0, 0, 2)
-            load_x(u, 1, 0, 2)
+        def load_x(s, q0, q1):
+            part, i0 = tile_rows(s, q0)
+            xt = keep.tile([P, q1 - q0, K], BF16, name="x%d_%d" % (s, q0))
+            rows = (re, im)[part][s // 2].rearrange("(p i) k -> p i k", i=4)
+            nc.sync.dma_start(out=xt[:], in_=rows[:, i0 : i0 + q1 - q0, :])
+            for q in range(q0, q1):
+                words[s, q] = xt[:].bitcast(F32)[:, q - q0, :]
+                if q + 1 < q1:
+                    word_pairs[s, q] = xt[:].bitcast(F32)[:, q - q0 : q - q0 + 2, :]
+
+        def load_set(s):
+            load_x(s, 0, 2)
+            load_x(s, 2, 4)
 
         def load_v(c):
             nc.sync.dma_start(out=v_raw[c][:].bitcast(I32), in_=v_words[2 * c : 2 * c + 2].bitcast(I32).rearrange("g p b -> p g b"))
@@ -79,29 +86,29 @@ def tile_split_real_schrodinger_step_s14_kernel(tc, re, im, phase, v_words, v_sc
         nc.vector.memset(vs_raw[0][:].bitcast(I32), 0)
         nc.vector.memset(vs_raw[1][:].bitcast(I32), 0)
         make_identity(nc, ident[:])
-        nc.gpsimd.memset(u_plane[:].bitcast(I32), 0)
+        nc.vector.memset(u_plane[:].bitcast(I32), 0)
 
-        load_x(0, 0, 0, 1)
-        load_x(0, 0, 1, 2)
+        load_x(0, 0, 1)
+        load_x(0, 1, 2)
         load_v(0)
-        load_x(0, 1, 0, 1)
-        load_x(0, 1, 1, 2)
+        load_x(0, 2, 3)
+        load_x(0, 3, 4)
         load_plane(vs_raw[0], v_scales[0:2])
-        load_unit(1)
-        load_unit(2)
+        load_set(1)
+        load_set(2)
         load_v(1)
         load_plane(vs_raw[1], v_scales[2:8])
+        load_set(3)
+        load_set(4)
         load_u(0)
         load_plane(u_plane, u_scales)
-        load_unit(3)
         load_v(2)
-        load_unit(4)
-        load_u(1)
+        load_set(5)
+        load_set(6)
         load_v(3)
-        load_unit(5)
-        load_unit(6)
+        load_u(1)
+        load_set(7)
         load_u(2)
-        load_unit(7)
         load_u(3)
 
         theta_flat = theta[:].rearrange("p c t -> p (c t)")
@@ -138,12 +145,14 @@ def tile_split_real_schrodinger_step_s14_kernel(tc, re, im, phase, v_words, v_sc
 
         sorted_words = {}
 
-        def sort_words(u, q):
-            w = work.tile([P, 512], F32, name="sorted_words", bufs=8)
-            sorted_words[u, q] = w
-            nc.vector.tensor_copy(
-                out=w[:].rearrange("p (g e r) -> p g e r", g=2, e=2),
-                in_=words[u, q].rearrange("p (g r e) -> p g e r", g=2, e=2),
+        def sort_pair(s, q, engine):
+            w = work.tile([P, 2, 512], F32, name="sorted_words", bufs=4)
+            sorted_words[s, q] = w[:, 0, :]
+            sorted_words[s, q + 1] = w[:, 1, :]
+            copy_on(
+                engine,
+                w[:].rearrange("p j (g e r) -> p (j g) e r", g=2, e=2),
+                word_pairs[s, q].rearrange("p j (g r e) -> p (j g) e r", g=2, e=2),
             )
 
         def turn(u, q):
@@ -164,8 +173,8 @@ def tile_split_real_schrodinger_step_s14_kernel(tc, re, im, phase, v_words, v_sc
         def turn_out(u, q, engine):
             if u not in grouped:
                 grouped[u] = work.tile([P, 2, 2048], BF16, name="grouped", bufs=2, align_bytes=256)
-                codes[u] = work.tile([P, 2, 512], U32, name="codes", bufs=3, align_bytes=256)
-                scales[u] = work.tile([P, 2, 512], U8, name="scales", bufs=3, align_bytes=256)
+                codes[u] = work.tile([P, 2, 512], U32, name="codes", bufs=4, align_bytes=256)
+                scales[u] = work.tile([P, 2, 512], U8, name="scales", bufs=4, align_bytes=256)
             dst = grouped[u][:].bitcast(F32).rearrange("p g (n e) -> p g n e", e=2)[:, :, 128 * q : 128 * (q + 1), :]
             copy_on(engine, dst, banks["T", u, q][:].rearrange("p (g e r) -> p g r e", g=2, e=2))
 
@@ -175,15 +184,21 @@ def tile_split_real_schrodinger_step_s14_kernel(tc, re, im, phase, v_words, v_sc
                 out=codes[u][:, g, cols].bitcast(FP8X4), scales=scales[u][:, g, cols], in_=grouped[u][:, g, 512 * q0 : 512 * q1]
             )
 
-        def deal_codes(c, g):
-            nc.vector.tensor_copy(
-                out=v_dealt[c][:].bitcast(U16)[:, g, :, :],
-                in_=v_raw[c][:].bitcast(U16)[:, g, :].rearrange("p (m t) -> p t m", t=4),
+        def quantize_set(s):
+            nc.vector.quantize_mx(
+                out=codes[s][:].rearrange("p g n -> p (g n)").bitcast(FP8X4),
+                scales=scales[s][:].rearrange("p g n -> p (g n)"),
+                in_=grouped[s][:].rearrange("p g n -> p (g n)"),
             )
 
-        def deal_scales(c, g):
-            raw = vs_raw[0][:, g, :] if c == 0 else vs_raw[1][:, 2 * (c - 1) + g, :]
-            nc.vector.tensor_copy(out=vs_dealt[c][:, g, :, :], in_=raw.rearrange("p (m t) -> p t m", t=4))
+        def deal_codes(c):
+            nc.vector.tensor_copy(
+                out=v_dealt[c][:].bitcast(U16), in_=v_raw[c][:].bitcast(U16).rearrange("p g (m t) -> p g t m", t=4)
+            )
+
+        def deal_scales(c):
+            raw = vs_raw[0][:] if c == 0 else vs_raw[1][:, 2 * (c - 1) : 2 * c, :]
+            nc.vector.tensor_copy(out=vs_dealt[c][:], in_=raw.rearrange("p g (m t) -> p g t m", t=4))
 
         def project(u, t):
             c = u // 2
@@ -205,170 +220,211 @@ def tile_split_real_schrodinger_step_s14_kernel(tc, re, im, phase, v_words, v_sc
         z_codes = {}
         z_scales = {}
 
-        def real_part(u, t):
-            a_cos[u, t] = work.tile([P, 256], F32, name="a_cos", bufs=4)
-            col = 4 * (u // 2) + t
-            nc.scalar.activation(out=a_cos[u, t][:], in_=banks["AB", u, t][:, 0:256], func=ACT.Copy, scale=trig[:, 1, col : col + 1])
+        def amplitude_cols(s):
+            if s // 2 < LAST:
+                return slice(0, 512), slice(0, 512), slice(0, 512)
+            return slice(0, 256), slice(256, 512), slice(256 * (s % 2), 256 * (s % 2 + 1))
 
-        def add_imag(u, t):
-            if u not in z_rows:
-                z_rows[u] = work.tile([P, 4, 256], BF16, name="z_rows", bufs=2)
-                z_grouped[u] = work.tile([P, 256, 4], BF16, name="z_grouped", bufs=2, align_bytes=256)
-                z_codes[u] = work.tile([P, 256], U32, name="z_codes", bufs=2, align_bytes=256)
-                z_scales[u] = work.tile([P, 256], U8, name="z_scales", bufs=2, align_bytes=256)
-            col = 4 * (u // 2) + t
+        def real_part(s, t):
+            c = s // 2
+            if (c, t) not in a_cos:
+                a_cos[c, t] = work.tile([P, 512], F32, name="a_cos", bufs=5)
+            a_cols, b_cols, cols = amplitude_cols(s)
+            nc.scalar.activation(
+                out=a_cos[c, t][:, cols], in_=banks["AB", s, t][:, a_cols], func=ACT.Copy, scale=trig[:, 1, 4 * c + t : 4 * c + t + 1]
+            )
+
+        def add_imag(s, t):
+            c = s // 2
+            if c not in z_rows:
+                z_rows[c] = work.tile([P, 4, 512], BF16, name="z_rows", bufs=2)
+                z_grouped[c] = work.tile([P, 512, 4], BF16, name="z_grouped", bufs=2, align_bytes=256)
+                z_codes[c] = work.tile([P, 512], U32, name="z_codes", bufs=2, align_bytes=256)
+                z_scales[c] = work.tile([P, 512], U8, name="z_scales", bufs=2, align_bytes=256)
+            a_cols, b_cols, cols = amplitude_cols(s)
             nc.vector.scalar_tensor_tensor(
-                out=z_rows[u][:, t, :], in0=banks["AB", u, t][:, 256:512], scalar=trig[:, 0, col : col + 1], in1=a_cos[u, t][:],
-                op0=ALU.mult, op1=ALU.add,
+                out=z_rows[c][:, t, cols], in0=banks["AB", s, t][:, b_cols], scalar=trig[:, 0, 4 * c + t : 4 * c + t + 1],
+                in1=a_cos[c, t][:, cols], op0=ALU.mult, op1=ALU.add,
             )
 
-        def interleave(u, j0, j1):
-            cols = slice(128 * j0, 128 * j1)
-            nc.vector.tensor_copy(out=z_grouped[u][:, cols, :], in_=z_rows[u][:, :, cols].rearrange("p t n -> p n t"))
+        def interleave(c, i0, i1):
+            cols = slice(128 * i0, 128 * i1)
+            nc.vector.tensor_copy(out=z_grouped[c][:, cols, :], in_=z_rows[c][:, :, cols].rearrange("p t n -> p n t"))
 
-        def quantize_z(u, j0, j1):
-            cols = slice(128 * j0, 128 * j1)
+        def quantize_z(c, i0, i1):
+            cols = slice(128 * i0, 128 * i1)
             nc.vector.quantize_mx(
-                out=z_codes[u][:, cols].bitcast(FP8X4), scales=z_scales[u][:, cols],
-                in_=z_grouped[u][:, cols, :].rearrange("p n t -> p (n t)"),
+                out=z_codes[c][:, cols].bitcast(FP8X4), scales=z_scales[c][:, cols],
+                in_=z_grouped[c][:, cols, :].rearrange("p n t -> p (n t)"),
             )
 
-        def expand(u, j, n):
-            c = u // 2
-            cols = slice(128 * j, 128 * (j + 1))
-            b = new_bank(("O", u, j, n))
+        def expand(c, i, n):
+            cols = slice(128 * i, 128 * (i + 1))
+            b = new_bank(("O", c, i, n))
             nc.tensor.matmul_mx(
                 out=b[:],
-                lhsT=z_codes[u][:, cols].bitcast(FP8X4),
-                lhsT_scale=z_scales[u][:, cols],
+                lhsT=z_codes[c][:, cols].bitcast(FP8X4),
+                lhsT_scale=z_scales[c][:, cols],
                 rhs=u_codes[c][:, 1024 * n : 1024 * (n + 1)].bitcast(FP4X4),
                 rhs_scale=u_plane[:, c, 512 * n : 512 * (n + 1)],
                 start=True,
                 stop=True,
             )
 
+        def expand_half(c, h):
+            for i in (2 * h, 2 * h + 1):
+                for n in range(2):
+                    expand(c, i, n)
+
         out_rows = {}
+        copied = []
 
-        def expand_out(u, j, n, engine):
-            c, h = divmod(u, 2)
-            if (u, j) not in out_rows:
-                out_rows[u, j] = work.tile([P, 1024], F32, name="out_rows", bufs=8)
+        def expand_out(c, i, n, engine):
+            if (c, i) not in out_rows:
+                out_rows[c, i] = work.tile([P, 1024], F32, name="out_rows", bufs=8)
             cols = slice(512 * n, 512 * (n + 1))
-            copy_on(engine, out_rows[u, j][:, cols], banks["O", u, j, n][:])
-            dst = out[c].rearrange("(p i) n -> p i n", i=4)[:, 2 * h + j, :]
-            if u == UNITS - 1 and j == 1:
-                nc.sync.dma_start(out=dst[:, cols], in_=out_rows[u, j][:, cols])
-            elif n == 1:
-                nc.sync.dma_start(out=dst, in_=out_rows[u, j][:])
+            copy_on(engine, out_rows[c, i][:, cols], banks["O", c, i, n][:])
+            copied.append((c, i, n))
+            dst = out[c].rearrange("(p i) n -> p i n", i=4)[:, i, :]
+            if c == LAST and i == 3:
+                nc.sync.dma_start(out=dst[:, cols], in_=out_rows[c, i][:, cols])
+            elif (c, i, 1 - n) in copied:
+                nc.sync.dma_start(out=dst, in_=out_rows[c, i][:])
 
-        def deal(piece):
-            c, half = divmod(piece, 4)
-            (deal_codes, deal_scales)[half % 2](c, half // 2)
+        def row_out(c, i, engine):
+            expand_out(c, i, 0, engine)
+            expand_out(c, i, 1, engine)
 
-        def project_out(u, t):
-            project(u, t)
-            real_part(u, t)
+        def turn_set(s):
+            for q in range(4):
+                turn(s, q)
 
         trig_reduce()
         turn(0, 0)
         turn(0, 1)
-        deal_codes(0, 0)
+        deal_codes(0)
         trig_square()
-        deal_codes(0, 1)
-        trig_finish()
         turn_out(0, 0, "scalar")
         turn_out(0, 1, "scalar")
         quantize_x(0, 0, 0, 2)
+        trig_finish()
         quantize_x(0, 1, 0, 2)
         turn(0, 2)
         turn_out(0, 2, "scalar")
-        deal_scales(0, 0)
-        quantize_x(0, 0, 2, 3)
-        quantize_x(0, 1, 2, 3)
         turn(0, 3)
         turn_out(0, 3, "scalar")
-        deal_scales(0, 1)
-        quantize_x(0, 0, 3, 4)
-        quantize_x(0, 1, 3, 4)
+        deal_scales(0)
+        quantize_x(0, 0, 2, 4)
+        quantize_x(0, 1, 2, 4)
         for q in (0, 1):
             turn(1, q)
             turn_out(1, q, "scalar")
-        sort_words(1, 2)
-        sort_words(1, 3)
-        project_out(0, 0)
-        sort_words(2, 0)
-        sort_words(2, 1)
-        add_imag(0, 0)
-        project_out(0, 1)
-        sort_words(2, 2)
-        sort_words(2, 3)
-        add_imag(0, 1)
+        sort_pair(1, 2, "vector")
+        for t in (0, 1):
+            project(0, t)
+            real_part(0, t)
+        sort_pair(2, 0, "vector")
+        sort_pair(2, 2, "vector")
+        deal_codes(1)
         for q in (2, 3):
             turn(1, q)
-            turn_out(1, q, "scalar")
-        deal(4)
-        deal(6)
-        project_out(0, 2)
-        quantize_x(1, 0)
-        add_imag(0, 2)
-        project_out(0, 3)
-        quantize_x(1, 1)
-        add_imag(0, 3)
+        turn_out(1, 2, "scalar")
+        turn_out(1, 3, "scalar")
+        deal_scales(1)
+        quantize_set(1)
+        for t in (2, 3):
+            project(0, t)
+            real_part(0, t)
 
-        pending = []
-        for k in range(1, UNITS):
-            ahead = k + 1 < UNITS
-            sorting = (0, 2, 1, 3)[: SORTED[k + 2] if k + 2 < UNITS else 0]
-            dealing = DEALS[k]
-            if ahead:
-                for q in (0, 1):
-                    turn(k + 1, q)
-            for j, n in pending:
-                expand_out(k - 2, j, n, "vector")
-            interleave(k - 1, 0, 2)
-            for q in sorting[:1]:
-                sort_words(k + 2, q)
-            quantize_z(k - 1, 0, 2)
-            if ahead:
-                for q in (0, 1):
-                    turn_out(k + 1, q, "scalar")
-            project_out(k, 0)
-            add_imag(k, 0)
-            for piece in dealing[:1]:
-                deal(piece)
-            project_out(k, 1)
-            add_imag(k, 1)
-            if ahead:
-                for q in (2, 3):
-                    turn(k + 1, q)
-                    turn_out(k + 1, q, "scalar")
-            for q in sorting[1:]:
-                sort_words(k + 2, q)
-            for piece in dealing[1:]:
-                deal(piece)
-            project_out(k, 2)
-            if ahead:
-                quantize_x(k + 1, 0)
-            add_imag(k, 2)
-            project_out(k, 3)
-            if ahead:
-                quantize_x(k + 1, 1)
-            add_imag(k, 3)
-            blocks = [(j, n) for j in range(2) for n in range(2)]
-            pending = blocks[4 - ON_VECTOR[k] :]
-            for j, n in blocks:
-                expand(k - 1, j, n)
-                if (j, n) not in pending:
-                    expand_out(k - 1, j, n, "scalar")
+        turn_set(2)
+        for q in range(4):
+            turn_out(2, q, "scalar")
+        sort_pair(3, 0, "vector")
+        sort_pair(3, 2, "vector")
+        for t in (0, 1):
+            project(1, t)
+            add_imag(1, t)
+        turn_set(3)
+        quantize_set(2)
+        for q in range(4):
+            turn_out(3, q, "scalar")
+        project(1, 2)
+        add_imag(1, 2)
+        project(1, 3)
+        add_imag(1, 3)
+        quantize_set(3)
 
-        last = UNITS - 1
-        interleave(last, 0, 1)
-        interleave(last, 1, 2)
-        quantize_z(last, 0, 1)
-        quantize_z(last, 1, 2)
-        for j, n in pending:
-            expand_out(last - 1, j, n, "vector")
-        for j in range(2):
+        def step(c, h):
+            s = 2 * c + 2 + h
+            turn_set(s)
+            if h == 0:
+                interleave(c - 1, 0, 4)
+            if (c, h) != (1, 0):
+                expand_out(c - 2 + h, 3 - 2 * h, 0, ("scalar", "vector")[h])
+                expand_out(c - 2 + h, 3 - 2 * h, 1, "vector")
+            if h == 0:
+                quantize_z(c - 1, 0, 4)
+                sort_pair(s + 1, 0, "vector")
+            else:
+                deal_codes(c + 1)
+                deal_scales(c + 1)
+            for q in range(3):
+                turn_out(s, q, "scalar")
+            t = 2 * h
+            project(2 * c, t)
+            real_part(2 * c, t)
+            turn_out(s, 3, "scalar")
+            project(2 * c + 1, t)
+            add_imag(2 * c + 1, t)
+            quantize_set(s)
+            project(2 * c, t + 1)
+            real_part(2 * c, t + 1)
+            project(2 * c + 1, t + 1)
+            add_imag(2 * c + 1, t + 1)
+            expand_half(c - 1, h)
+            row_out(c - 1, 2 * h, "scalar")
+
+        for c in (1, 2):
+            for h in range(2):
+                step(c, h)
+
+        expand_out(1, 3, 0, "scalar")
+        interleave(2, 0, 2)
+        expand_out(1, 3, 1, "scalar")
+        quantize_z(2, 0, 2)
+        for t in range(4):
+            project(6, t)
+            real_part(6, t)
+            add_imag(6, t)
+            if t == 0:
+                interleave(2, 2, 4)
+            if t == 1:
+                quantize_z(2, 2, 4)
+        expand_half(2, 0)
+        row_out(2, 0, "scalar")
+        expand_out(2, 1, 0, "scalar")
+        interleave(LAST, 0, 2)
+        expand_out(2, 1, 1, "scalar")
+        quantize_z(LAST, 0, 2)
+        expand_half(2, 1)
+        expand_out(2, 2, 0, "scalar")
+        expand_out(2, 2, 1, "vector")
+        expand_out(2, 3, 0, "scalar")
+        expand_out(2, 3, 1, "vector")
+        for t in range(4):
+            project(7, t)
+            real_part(7, t)
+            add_imag(7, t)
+        expand_half(LAST, 0)
+        expand_out(LAST, 0, 0, "scalar")
+        expand_out(LAST, 0, 1, "scalar")
+        interleave(LAST, 2, 3)
+        interleave(LAST, 3, 4)
+        quantize_z(LAST, 2, 3)
+        quantize_z(LAST, 3, 4)
+        expand_out(LAST, 1, 0, "scalar")
+        expand_out(LAST, 1, 1, "scalar")
+        for i in (2, 3):
             for n in range(2):
-                expand(last, j, n)
-                expand_out(last, j, n, ("scalar", "vector")[n])
+                expand(LAST, i, n)
+                expand_out(LAST, i, n, ("scalar", "vector")[n])

@@ -151,8 +151,8 @@ def tile_split_real_schrodinger_step_s14_kernel(tc, re, im, phase, v_words, v_sc
             sorted_words[s, q + 1] = w[:, 1, :]
             copy_on(
                 engine,
-                w[:].rearrange("p j (g e r) -> p (j g) e r", g=2, e=2),
-                word_pairs[s, q].rearrange("p j (g r e) -> p (j g) e r", g=2, e=2),
+                w[:].rearrange("p j (g e b r) -> p (j g) b e r", g=2, e=2, r=8),
+                word_pairs[s, q].rearrange("p j (g b r e) -> p (j g) b e r", g=2, e=2, r=8),
             )
 
         def turn(u, q):
@@ -193,12 +193,16 @@ def tile_split_real_schrodinger_step_s14_kernel(tc, re, im, phase, v_words, v_sc
 
         def deal_codes(c):
             nc.vector.tensor_copy(
-                out=v_dealt[c][:].bitcast(U16), in_=v_raw[c][:].bitcast(U16).rearrange("p g (m t) -> p g t m", t=4)
+                out=v_dealt[c][:].bitcast(U16).rearrange("p g t (b m) -> p g b t m", m=8),
+                in_=v_raw[c][:].bitcast(U16).rearrange("p g (b m t) -> p g b t m", t=4, m=8),
             )
 
         def deal_scales(c):
             raw = vs_raw[0][:] if c == 0 else vs_raw[1][:, 2 * (c - 1) : 2 * c, :]
-            nc.vector.tensor_copy(out=vs_dealt[c][:], in_=raw.rearrange("p g (m t) -> p g t m", t=4))
+            nc.vector.tensor_copy(
+                out=vs_dealt[c][:].rearrange("p g t (b m) -> p g b t m", m=16),
+                in_=raw.rearrange("p g (b m t) -> p g b t m", t=4, m=16),
+            )
 
         def project(u, t):
             c = u // 2
@@ -249,7 +253,10 @@ def tile_split_real_schrodinger_step_s14_kernel(tc, re, im, phase, v_words, v_sc
 
         def interleave(c, i0, i1):
             cols = slice(128 * i0, 128 * i1)
-            nc.vector.tensor_copy(out=z_grouped[c][:, cols, :], in_=z_rows[c][:, :, cols].rearrange("p t n -> p n t"))
+            nc.vector.tensor_copy(
+                out=z_grouped[c][:, cols, :].rearrange("p (b n) t -> p b t n", n=4),
+                in_=z_rows[c][:, :, cols].rearrange("p t (b n) -> p b t n", n=4),
+            )
 
         def quantize_z(c, i0, i1):
             cols = slice(128 * i0, 128 * i1)
@@ -330,8 +337,8 @@ def tile_split_real_schrodinger_step_s14_kernel(tc, re, im, phase, v_words, v_sc
             turn(1, q)
         turn_out(1, 2, "scalar")
         turn_out(1, 3, "scalar")
-        deal_scales(1)
         quantize_set(1)
+        deal_scales(1)
         for t in (2, 3):
             project(0, t)
             real_part(0, t)
@@ -356,11 +363,12 @@ def tile_split_real_schrodinger_step_s14_kernel(tc, re, im, phase, v_words, v_sc
 
         def step(c, h):
             s = 2 * c + 2 + h
-            turn_set(s)
+            turn(s, 0)
+            turn(s, 1)
             if h == 0:
                 interleave(c - 1, 0, 4)
             if (c, h) != (1, 0):
-                expand_out(c - 2 + h, 3 - 2 * h, 0, ("scalar", "vector")[h])
+                expand_out(c - 2 + h, 3 - 2 * h, 0, "scalar")
                 expand_out(c - 2 + h, 3 - 2 * h, 1, "vector")
             if h == 0:
                 quantize_z(c - 1, 0, 4)
@@ -368,17 +376,21 @@ def tile_split_real_schrodinger_step_s14_kernel(tc, re, im, phase, v_words, v_sc
             else:
                 deal_codes(c + 1)
                 deal_scales(c + 1)
-            for q in range(3):
-                turn_out(s, q, "scalar")
+                if s + 1 < SETS:
+                    sort_pair(s + 1, 0, "vector")
             t = 2 * h
+            turn_out(s, 0, "scalar")
+            turn_out(s, 1, "scalar")
             project(2 * c, t)
             real_part(2 * c, t)
-            turn_out(s, 3, "scalar")
             project(2 * c + 1, t)
             add_imag(2 * c + 1, t)
-            quantize_set(s)
+            for q in (2, 3):
+                turn(s, q)
+                turn_out(s, q, "scalar")
             project(2 * c, t + 1)
             real_part(2 * c, t + 1)
+            quantize_set(s)
             project(2 * c + 1, t + 1)
             add_imag(2 * c + 1, t + 1)
             expand_half(c - 1, h)

@@ -57,7 +57,7 @@ def tile_split_real_schrodinger_step_s14_kernel(tc, re, im, phase, v_words, v_sc
 
         def load_x(s, q0, q1):
             part, i0 = tile_rows(s, q0)
-            xt = keep.tile([P, q1 - q0, K], BF16, name="x%d_%d" % (s, q0))
+            xt = work.tile([P, q1 - q0, K], BF16, name="rows", bufs=26)
             rows = (re, im)[part][s // 2].rearrange("(p i) k -> p i k", i=4)
             nc.sync.dma_start(out=xt[:], in_=rows[:, i0 : i0 + q1 - q0, :])
             for q in range(q0, q1):
@@ -288,7 +288,7 @@ def tile_split_real_schrodinger_step_s14_kernel(tc, re, im, phase, v_words, v_sc
 
         def expand_out(c, i, n, engine):
             if (c, i) not in out_rows:
-                out_rows[c, i] = work.tile([P, 1024], F32, name="out_rows", bufs=8)
+                out_rows[c, i] = work.tile([P, 1024], F32, name="rows", bufs=26)
             cols = slice(512 * n, 512 * (n + 1))
             copy_on(engine, out_rows[c, i][:, cols], banks["O", c, i, n][:])
             copied.append((c, i, n))
@@ -323,120 +323,136 @@ def tile_split_real_schrodinger_step_s14_kernel(tc, re, im, phase, v_words, v_sc
         deal_scales(0)
         quantize_x(0, 0, 2, 4)
         quantize_x(0, 1, 2, 4)
-        for q in (0, 1):
-            turn(1, q)
-            turn_out(1, q, "scalar")
+        turn(1, 0)
+        turn(1, 1)
+        turn_out(1, 0, "scalar")
+        turn_out(1, 1, "scalar")
         sort_pair(1, 2, "vector")
+        sort_pair(2, 0, "scalar")
         for t in (0, 1):
             project(0, t)
             real_part(0, t)
-        sort_pair(2, 0, "vector")
         sort_pair(2, 2, "vector")
         deal_codes(1)
-        for q in (2, 3):
-            turn(1, q)
-        turn_out(1, 2, "scalar")
+        turn(1, 2)
+        turn(1, 3)
+        turn_out(1, 2, "vector")
         turn_out(1, 3, "scalar")
         quantize_set(1)
-        deal_scales(1)
+        sort_pair(3, 0, "vector")
         for t in (2, 3):
             project(0, t)
             real_part(0, t)
-
         turn_set(2)
-        for q in range(4):
-            turn_out(2, q, "scalar")
-        sort_pair(3, 0, "vector")
         sort_pair(3, 2, "vector")
-        for t in (0, 1):
-            project(1, t)
-            add_imag(1, t)
-        turn_set(3)
+        turn_out(2, 1, "scalar")
+        turn_out(2, 0, "scalar")
+        turn_out(2, 2, "scalar")
+        turn_out(2, 3, "scalar")
+        project(1, 0)
+        add_imag(1, 0)
+        deal_scales(1)
+        project(1, 1)
+        add_imag(1, 1)
         quantize_set(2)
-        for q in range(4):
+        turn_set(3)
+        for q in (1, 0, 3, 2):
             turn_out(3, q, "scalar")
         project(1, 2)
         add_imag(1, 2)
+        quantize_set(3)
         project(1, 3)
         add_imag(1, 3)
-        quantize_set(3)
 
         def step(c, h):
             s = 2 * c + 2 + h
+            t = 2 * h
             turn(s, 0)
             turn(s, 1)
-            if h == 0:
-                interleave(c - 1, 0, 4)
             if (c, h) != (1, 0):
-                expand_out(c - 2 + h, 3 - 2 * h, 0, "scalar")
                 expand_out(c - 2 + h, 3 - 2 * h, 1, "vector")
+                expand_out(c - 2 + h, 3 - 2 * h, 0, "scalar")
+            turn_out(s, 1, "scalar")
+            turn_out(s, 0, "scalar")
             if h == 0:
-                quantize_z(c - 1, 0, 4)
+                interleave(c - 1, 0, 2)
                 sort_pair(s + 1, 0, "vector")
+                quantize_z(c - 1, 0, 2)
             else:
                 deal_codes(c + 1)
                 deal_scales(c + 1)
-                if s + 1 < SETS:
-                    sort_pair(s + 1, 0, "vector")
-            t = 2 * h
-            turn_out(s, 0, "scalar")
-            turn_out(s, 1, "scalar")
+                quantize_set(s - 1)
             project(2 * c, t)
             real_part(2 * c, t)
             project(2 * c + 1, t)
             add_imag(2 * c + 1, t)
-            for q in (2, 3):
-                turn(s, q)
-                turn_out(s, q, "scalar")
+            turn(s, 2)
+            turn(s, 3)
+            turn_out(s, 3, "scalar")
+            turn_out(s, 2, "scalar")
+            if h == 0:
+                interleave(c - 1, 2, 4)
+            elif s + 1 < SETS:
+                sort_pair(s + 1, 0, "vector")
             project(2 * c, t + 1)
             real_part(2 * c, t + 1)
-            quantize_set(s)
+            if h == 1:
+                quantize_set(s)
             project(2 * c + 1, t + 1)
             add_imag(2 * c + 1, t + 1)
+            if h == 0:
+                quantize_z(c - 1, 2, 4)
             expand_half(c - 1, h)
-            row_out(c - 1, 2 * h, "scalar")
+            expand_out(c - 1, 2 * h, 1, "scalar")
+            expand_out(c - 1, 2 * h, 0, "scalar")
 
         for c in (1, 2):
             for h in range(2):
                 step(c, h)
 
-        expand_out(1, 3, 0, "scalar")
         interleave(2, 0, 2)
         expand_out(1, 3, 1, "scalar")
+        expand_out(1, 3, 0, "scalar")
         quantize_z(2, 0, 2)
+        interleave(2, 2, 4)
         for t in range(4):
             project(6, t)
             real_part(6, t)
             add_imag(6, t)
-            if t == 0:
-                interleave(2, 2, 4)
             if t == 1:
                 quantize_z(2, 2, 4)
         expand_half(2, 0)
-        row_out(2, 0, "scalar")
-        expand_out(2, 1, 0, "scalar")
-        interleave(LAST, 0, 2)
+        expand_out(2, 0, 1, "scalar")
+        expand_out(2, 0, 0, "scalar")
         expand_out(2, 1, 1, "scalar")
-        quantize_z(LAST, 0, 2)
+        expand_out(2, 1, 0, "vector")
+        interleave(LAST, 0, 2)
+        project(7, 0)
+        project(7, 1)
         expand_half(2, 1)
-        expand_out(2, 2, 0, "scalar")
+        real_part(7, 0)
+        real_part(7, 1)
         expand_out(2, 2, 1, "vector")
-        expand_out(2, 3, 0, "scalar")
+        quantize_z(LAST, 0, 2)
+        add_imag(7, 0)
+        add_imag(7, 1)
+        expand_out(2, 2, 0, "scalar")
         expand_out(2, 3, 1, "vector")
-        for t in range(4):
+        expand_out(2, 3, 0, "scalar")
+        for t in (2, 3):
             project(7, t)
             real_part(7, t)
             add_imag(7, t)
         expand_half(LAST, 0)
-        expand_out(LAST, 0, 0, "scalar")
         expand_out(LAST, 0, 1, "scalar")
+        expand_out(LAST, 0, 0, "scalar")
         interleave(LAST, 2, 3)
         interleave(LAST, 3, 4)
         quantize_z(LAST, 2, 3)
         quantize_z(LAST, 3, 4)
-        expand_out(LAST, 1, 0, "scalar")
         expand_out(LAST, 1, 1, "scalar")
+        expand_out(LAST, 1, 0, "scalar")
         for i in (2, 3):
             for n in range(2):
                 expand(LAST, i, n)
-                expand_out(LAST, i, n, ("scalar", "vector")[n])
+                expand_out(LAST, i, n, ("vector", "scalar")[n])

@@ -95,17 +95,17 @@ def tile_split_real_schrodinger_step_s14_kernel(tc, re, im, phase, v_words, v_sc
         load_x(0, 3, 4)
         load_plane(vs_raw[0], v_scales[0:2])
         load_set(1)
-        load_set(2)
         load_v(1)
         load_plane(vs_raw[1], v_scales[2:8])
+        load_set(2)
+        load_v(2)
         load_set(3)
         load_set(4)
+        load_v(3)
         load_u(0)
         load_plane(u_plane, u_scales)
-        load_v(2)
         load_set(5)
         load_set(6)
-        load_v(3)
         load_u(1)
         load_set(7)
         load_u(2)
@@ -242,7 +242,6 @@ def tile_split_real_schrodinger_step_s14_kernel(tc, re, im, phase, v_words, v_sc
             c = s // 2
             if c not in z_rows:
                 z_rows[c] = work.tile([P, 4, 512], BF16, name="z_rows", bufs=2)
-                z_grouped[c] = work.tile([P, 512, 4], BF16, name="z_grouped", bufs=2, align_bytes=256)
                 z_codes[c] = work.tile([P, 512], U32, name="z_codes", bufs=2, align_bytes=256)
                 z_scales[c] = work.tile([P, 512], U8, name="z_scales", bufs=2, align_bytes=256)
             a_cols, b_cols, cols = amplitude_cols(s)
@@ -253,8 +252,10 @@ def tile_split_real_schrodinger_step_s14_kernel(tc, re, im, phase, v_words, v_sc
 
         def interleave(c, i0, i1):
             cols = slice(128 * i0, 128 * i1)
+            zt = work.tile([P, 128 * (i1 - i0), 4], BF16, name="z_grouped", bufs=3, align_bytes=256)
+            z_grouped[c, i0] = zt
             nc.vector.tensor_copy(
-                out=z_grouped[c][:, cols, :].rearrange("p (b n) t -> p b t n", n=4),
+                out=zt[:].rearrange("p (b n) t -> p b t n", n=4),
                 in_=z_rows[c][:, :, cols].rearrange("p t (b n) -> p b t n", n=4),
             )
 
@@ -262,7 +263,7 @@ def tile_split_real_schrodinger_step_s14_kernel(tc, re, im, phase, v_words, v_sc
             cols = slice(128 * i0, 128 * i1)
             nc.vector.quantize_mx(
                 out=z_codes[c][:, cols].bitcast(FP8X4), scales=z_scales[c][:, cols],
-                in_=z_grouped[c][:, cols, :].rearrange("p n t -> p (n t)"),
+                in_=z_grouped[c, i0][:].rearrange("p n t -> p (n t)"),
             )
 
         def expand(c, i, n):
@@ -328,121 +329,153 @@ def tile_split_real_schrodinger_step_s14_kernel(tc, re, im, phase, v_words, v_sc
         turn_out(1, 0, "scalar")
         turn_out(1, 1, "scalar")
         sort_pair(1, 2, "vector")
-        sort_pair(2, 0, "scalar")
+        deal_codes(1)
+        deal_scales(1)
         for t in (0, 1):
             project(0, t)
             real_part(0, t)
+        sort_pair(2, 0, "vector")
         sort_pair(2, 2, "vector")
-        deal_codes(1)
         turn(1, 2)
         turn(1, 3)
         turn_out(1, 2, "vector")
         turn_out(1, 3, "scalar")
         quantize_set(1)
         sort_pair(3, 0, "vector")
-        for t in (2, 3):
-            project(0, t)
-            real_part(0, t)
-        turn_set(2)
-        sort_pair(3, 2, "vector")
+        project(0, 2)
+        real_part(0, 2)
+        turn(2, 0)
+        turn(2, 1)
+        project(0, 3)
+        real_part(0, 3)
         turn_out(2, 1, "scalar")
         turn_out(2, 0, "scalar")
-        turn_out(2, 2, "scalar")
+        turn(2, 2)
+        turn(2, 3)
+        sort_pair(3, 2, "vector")
         turn_out(2, 3, "scalar")
+        turn_out(2, 2, "scalar")
         project(1, 0)
         add_imag(1, 0)
-        deal_scales(1)
+        deal_codes(2)
         project(1, 1)
         add_imag(1, 1)
+        turn(3, 0)
+        turn(3, 1)
+        turn_out(3, 1, "scalar")
+        turn_out(3, 0, "scalar")
         quantize_set(2)
-        turn_set(3)
-        for q in (1, 0, 3, 2):
-            turn_out(3, q, "scalar")
         project(1, 2)
         add_imag(1, 2)
-        quantize_set(3)
+        turn(3, 2)
+        turn(3, 3)
+        turn_out(3, 3, "scalar")
+        turn_out(3, 2, "scalar")
         project(1, 3)
         add_imag(1, 3)
+        quantize_set(3)
 
-        def step(c, h):
-            s = 2 * c + 2 + h
-            t = 2 * h
+        def real_step(c):
+            s = 2 * c + 2
             turn(s, 0)
             turn(s, 1)
-            if (c, h) != (1, 0):
-                expand_out(c - 2 + h, 3 - 2 * h, 1, "vector")
-                expand_out(c - 2 + h, 3 - 2 * h, 0, "scalar")
+            interleave(c - 1, 0, 2)
+            if c > 1:
+                expand_out(c - 2, 3, 1, "vector")
+                expand_out(c - 2, 3, 0, "scalar")
             turn_out(s, 1, "scalar")
             turn_out(s, 0, "scalar")
-            if h == 0:
-                interleave(c - 1, 0, 2)
-                sort_pair(s + 1, 0, "vector")
-                quantize_z(c - 1, 0, 2)
-            else:
-                deal_codes(c + 1)
-                deal_scales(c + 1)
-                quantize_set(s - 1)
-            project(2 * c, t)
-            real_part(2 * c, t)
-            project(2 * c + 1, t)
-            add_imag(2 * c + 1, t)
+            sort_pair(s + 1, 0, "vector")
+            quantize_z(c - 1, 0, 2)
+            project(2 * c, 0)
+            real_part(2 * c, 0)
+            project(2 * c, 1)
+            real_part(2 * c, 1)
+            interleave(c - 1, 2, 4)
             turn(s, 2)
             turn(s, 3)
             turn_out(s, 3, "scalar")
             turn_out(s, 2, "scalar")
-            if h == 0:
-                interleave(c - 1, 2, 4)
-            elif s + 1 < SETS:
-                sort_pair(s + 1, 0, "vector")
-            project(2 * c, t + 1)
-            real_part(2 * c, t + 1)
-            if h == 1:
-                quantize_set(s)
-            project(2 * c + 1, t + 1)
-            add_imag(2 * c + 1, t + 1)
-            if h == 0:
-                quantize_z(c - 1, 2, 4)
-            expand_half(c - 1, h)
-            expand_out(c - 1, 2 * h, 1, "scalar")
-            expand_out(c - 1, 2 * h, 0, "scalar")
+            deal_scales(c + 1)
+            project(2 * c + 1, 0)
+            add_imag(2 * c + 1, 0)
+            project(2 * c + 1, 1)
+            add_imag(2 * c + 1, 1)
+            quantize_z(c - 1, 2, 4)
+            expand_half(c - 1, 0)
+            expand_out(c - 1, 0, 1, "scalar")
+            expand_out(c - 1, 0, 0, "scalar")
+
+        def imag_step(c):
+            s = 2 * c + 3
+            turn(s, 0)
+            turn(s, 1)
+            expand_out(c - 1, 1, 1, "vector")
+            expand_out(c - 1, 1, 0, "scalar")
+            turn_out(s, 1, "scalar")
+            turn_out(s, 0, "scalar")
+            if c == 1:
+                deal_codes(3)
+            quantize_set(s - 1)
+            project(2 * c, 2)
+            real_part(2 * c, 2)
+            project(2 * c + 1, 2)
+            add_imag(2 * c + 1, 2)
+            turn(s, 2)
+            turn(s, 3)
+            turn_out(s, 3, ("scalar", "vector")[c - 1])
+            turn_out(s, 2, "scalar")
+            project(2 * c, 3)
+            real_part(2 * c, 3)
+            project(2 * c + 1, 3)
+            add_imag(2 * c + 1, 3)
+            quantize_set(s)
+            expand_half(c - 1, 1)
+            expand_out(c - 1, 2, 1, "scalar")
+            expand_out(c - 1, 2, 0, "scalar")
 
         for c in (1, 2):
-            for h in range(2):
-                step(c, h)
+            real_step(c)
+            imag_step(c)
 
-        interleave(2, 0, 2)
         expand_out(1, 3, 1, "scalar")
         expand_out(1, 3, 0, "scalar")
-        quantize_z(2, 0, 2)
+        interleave(2, 0, 2)
         interleave(2, 2, 4)
+        quantize_z(2, 0, 2)
         for t in range(4):
             project(6, t)
             real_part(6, t)
             add_imag(6, t)
-            if t == 1:
+            if t == 0:
                 quantize_z(2, 2, 4)
         expand_half(2, 0)
         expand_out(2, 0, 1, "scalar")
         expand_out(2, 0, 0, "scalar")
-        expand_out(2, 1, 1, "scalar")
+        expand_out(2, 1, 1, "vector")
         expand_out(2, 1, 0, "vector")
         interleave(LAST, 0, 2)
         project(7, 0)
-        project(7, 1)
-        expand_half(2, 1)
         real_part(7, 0)
-        real_part(7, 1)
-        expand_out(2, 2, 1, "vector")
-        quantize_z(LAST, 0, 2)
         add_imag(7, 0)
-        add_imag(7, 1)
+        quantize_z(LAST, 0, 2)
+        expand(2, 2, 0)
+        expand(2, 2, 1)
+        expand_out(2, 2, 1, "scalar")
         expand_out(2, 2, 0, "scalar")
+        project(7, 1)
+        real_part(7, 1)
+        add_imag(7, 1)
+        expand(2, 3, 0)
+        expand(2, 3, 1)
         expand_out(2, 3, 1, "vector")
         expand_out(2, 3, 0, "scalar")
-        for t in (2, 3):
-            project(7, t)
-            real_part(7, t)
-            add_imag(7, t)
+        project(7, 2)
+        real_part(7, 2)
+        add_imag(7, 2)
+        project(7, 3)
+        real_part(7, 3)
+        add_imag(7, 3)
         expand_half(LAST, 0)
         expand_out(LAST, 0, 1, "scalar")
         expand_out(LAST, 0, 0, "scalar")

@@ -255,8 +255,8 @@ def tile_split_real_schrodinger_step_s14_kernel(tc, re, im, phase, v_words, v_sc
             zt = work.tile([P, 128 * (i1 - i0), 4], BF16, name="z_grouped", bufs=3, align_bytes=256)
             z_grouped[c, i0] = zt
             nc.vector.tensor_copy(
-                out=zt[:].rearrange("p (b n) t -> p b t n", n=4),
-                in_=z_rows[c][:, :, cols].rearrange("p t (b n) -> p b t n", n=4),
+                out=zt[:],
+                in_=z_rows[c][:, :, cols].rearrange("p t n -> p n t"),
             )
 
         def quantize_z(c, i0, i1):

@@ -33,7 +33,7 @@ def tile_split_real_schrodinger_step_s14_kernel(tc, re, im, phase, v_words, v_sc
 
         v_raw = [keep.tile([P, 2, 1024], U8, name="v_raw%d" % c, align_bytes=256) for c in range(G)]
         v_dealt = [keep.tile([P, 2, 4, 256], U8, name="v_dealt%d" % c, align_bytes=256) for c in range(G)]
-        vs_raw = [keep.tile([P, 2, 512], U8, name="vs_raw0", align_bytes=256), keep.tile([P, 6, 512], U8, name="vs_raw1", align_bytes=256)]
+        vs_raw = keep.tile([P, 2 * G, 512], U8, name="vs_raw", align_bytes=256)
         vs_dealt = [keep.tile([P, 2, 4, 128], U8, name="vs_dealt%d" % c, align_bytes=256) for c in range(G)]
         u_codes = [keep.tile([P, 2048], U8, name="u_codes%d" % c, align_bytes=256) for c in range(G)]
         u_plane = keep.tile([P, G, 1024], U8, name="u_plane", align_bytes=256)
@@ -57,7 +57,7 @@ def tile_split_real_schrodinger_step_s14_kernel(tc, re, im, phase, v_words, v_sc
 
         def load_x(s, q0, q1):
             part, i0 = tile_rows(s, q0)
-            xt = work.tile([P, q1 - q0, K], BF16, name="rows", bufs=26)
+            xt = work.tile([P, q1 - q0, K], BF16, name="rows", bufs=24)
             rows = (re, im)[part][s // 2].rearrange("(p i) k -> p i k", i=4)
             nc.sync.dma_start(out=xt[:], in_=rows[:, i0 : i0 + q1 - q0, :])
             for q in range(q0, q1):
@@ -83,33 +83,29 @@ def tile_split_real_schrodinger_step_s14_kernel(tc, re, im, phase, v_words, v_sc
                 )
 
         nc.scalar.dma_start(out=theta[:], in_=phase.rearrange("c (p t) -> p c t", t=4))
-        nc.vector.memset(vs_raw[0][:].bitcast(I32), 0)
-        nc.vector.memset(vs_raw[1][:].bitcast(I32), 0)
+        nc.vector.memset(vs_raw[:].bitcast(I32), 0)
         make_identity(nc, ident[:])
         nc.vector.memset(u_plane[:].bitcast(I32), 0)
 
         load_x(0, 0, 1)
         load_x(0, 1, 2)
-        load_v(0)
-        load_x(0, 2, 3)
-        load_x(0, 3, 4)
-        load_plane(vs_raw[0], v_scales[0:2])
+        load_x(0, 2, 4)
         load_set(1)
-        load_v(1)
-        load_plane(vs_raw[1], v_scales[2:8])
+        load_v(0)
+        load_plane(vs_raw, v_scales)
         load_set(2)
-        load_v(2)
         load_set(3)
+        load_v(1)
         load_set(4)
+        load_v(2)
+        load_set(5)
         load_v(3)
+        load_set(6)
         load_u(0)
         load_plane(u_plane, u_scales)
-        load_set(5)
-        load_set(6)
-        load_u(1)
         load_set(7)
-        load_u(2)
-        load_u(3)
+        for c in range(1, G):
+            load_u(c)
 
         theta_flat = theta[:].rearrange("p c t -> p (c t)")
 
@@ -173,8 +169,8 @@ def tile_split_real_schrodinger_step_s14_kernel(tc, re, im, phase, v_words, v_sc
         def turn_out(u, q, engine):
             if u not in grouped:
                 grouped[u] = work.tile([P, 2, 2048], BF16, name="grouped", bufs=2, align_bytes=256)
-                codes[u] = work.tile([P, 2, 512], U32, name="codes", bufs=4, align_bytes=256)
-                scales[u] = work.tile([P, 2, 512], U8, name="scales", bufs=4, align_bytes=256)
+                codes[u] = work.tile([P, 2, 512], U32, name="codes", bufs=6, align_bytes=256)
+                scales[u] = work.tile([P, 2, 512], U8, name="scales", bufs=6, align_bytes=256)
             dst = grouped[u][:].bitcast(F32).rearrange("p g (n e) -> p g n e", e=2)[:, :, 128 * q : 128 * (q + 1), :]
             copy_on(engine, dst, banks["T", u, q][:].rearrange("p (g e r) -> p g r e", g=2, e=2))
 
@@ -198,7 +194,7 @@ def tile_split_real_schrodinger_step_s14_kernel(tc, re, im, phase, v_words, v_sc
             )
 
         def deal_scales(c):
-            raw = vs_raw[0][:] if c == 0 else vs_raw[1][:, 2 * (c - 1) : 2 * c, :]
+            raw = vs_raw[:, 2 * c : 2 * c + 2, :]
             nc.vector.tensor_copy(
                 out=vs_dealt[c][:].rearrange("p g t (b m) -> p g b t m", m=16),
                 in_=raw.rearrange("p g (b m t) -> p g b t m", t=4, m=16),
@@ -229,14 +225,19 @@ def tile_split_real_schrodinger_step_s14_kernel(tc, re, im, phase, v_words, v_sc
                 return slice(0, 512), slice(0, 512), slice(0, 512)
             return slice(0, 256), slice(256, 512), slice(256 * (s % 2), 256 * (s % 2 + 1))
 
-        def real_part(s, t):
+        def real_part(s, t, engine="scalar"):
             c = s // 2
             if (c, t) not in a_cos:
                 a_cos[c, t] = work.tile([P, 512], F32, name="a_cos", bufs=5)
             a_cols, b_cols, cols = amplitude_cols(s)
-            nc.scalar.activation(
-                out=a_cos[c, t][:, cols], in_=banks["AB", s, t][:, a_cols], func=ACT.Copy, scale=trig[:, 1, 4 * c + t : 4 * c + t + 1]
-            )
+            if engine == "vector":
+                nc.vector.tensor_scalar(
+                    out=a_cos[c, t][:, cols], in0=banks["AB", s, t][:, a_cols], scalar1=trig[:, 1, 4 * c + t : 4 * c + t + 1], scalar2=None, op0=ALU.mult
+                )
+            else:
+                nc.scalar.activation(
+                    out=a_cos[c, t][:, cols], in_=banks["AB", s, t][:, a_cols], func=ACT.Copy, scale=trig[:, 1, 4 * c + t : 4 * c + t + 1]
+                )
 
         def add_imag(s, t):
             c = s // 2
@@ -250,13 +251,14 @@ def tile_split_real_schrodinger_step_s14_kernel(tc, re, im, phase, v_words, v_sc
                 in1=a_cos[c, t][:, cols], op0=ALU.mult, op1=ALU.add,
             )
 
-        def interleave(c, i0, i1):
+        def interleave(c, i0, i1, engine="vector"):
             cols = slice(128 * i0, 128 * i1)
             zt = work.tile([P, 128 * (i1 - i0), 4], BF16, name="z_grouped", bufs=3, align_bytes=256)
             z_grouped[c, i0] = zt
-            nc.vector.tensor_copy(
-                out=zt[:],
-                in_=z_rows[c][:, :, cols].rearrange("p t n -> p n t"),
+            copy_on(
+                engine,
+                zt[:].rearrange("p (b n) t -> p b t n", n=4),
+                z_rows[c][:, :, cols].rearrange("p t (b n) -> p b t n", n=4),
             )
 
         def quantize_z(c, i0, i1):
@@ -289,7 +291,7 @@ def tile_split_real_schrodinger_step_s14_kernel(tc, re, im, phase, v_words, v_sc
 
         def expand_out(c, i, n, engine):
             if (c, i) not in out_rows:
-                out_rows[c, i] = work.tile([P, 1024], F32, name="rows", bufs=26)
+                out_rows[c, i] = work.tile([P, 1024], F32, name="rows", bufs=24)
             cols = slice(512 * n, 512 * (n + 1))
             copy_on(engine, out_rows[c, i][:, cols], banks["O", c, i, n][:])
             copied.append((c, i, n))
@@ -307,136 +309,112 @@ def tile_split_real_schrodinger_step_s14_kernel(tc, re, im, phase, v_words, v_sc
             for q in range(4):
                 turn(s, q)
 
+        def turn_pair(s, q, first="scalar", second="scalar"):
+            turn(s, q)
+            turn(s, q + 1)
+            turn_out(s, q + 1, first)
+            turn_out(s, q, second)
+
+        def real_pair(s, t):
+            project(s, t)
+            project(s, t + 1)
+            real_part(s, t)
+            real_part(s, t + 1)
+
+        def imag_pair(s, t):
+            for j in range(2):
+                project(s, t + j)
+                add_imag(s, t + j)
+
         trig_reduce()
         turn(0, 0)
-        turn(0, 1)
-        deal_codes(0)
-        trig_square()
         turn_out(0, 0, "scalar")
-        turn_out(0, 1, "scalar")
-        quantize_x(0, 0, 0, 2)
+        trig_square()
+        turn(0, 1)
+        turn_out(0, 1, "vector")
         trig_finish()
-        quantize_x(0, 1, 0, 2)
-        turn(0, 2)
-        turn_out(0, 2, "scalar")
-        turn(0, 3)
-        turn_out(0, 3, "scalar")
+        turn_pair(0, 2, "scalar", "vector")
+        quantize_set(0)
+        turn_pair(1, 0)
+        deal_codes(0)
+        turn_pair(1, 2, "scalar", "scalar")
         deal_scales(0)
-        quantize_x(0, 0, 2, 4)
-        quantize_x(0, 1, 2, 4)
-        turn(1, 0)
-        turn(1, 1)
-        turn_out(1, 0, "scalar")
-        turn_out(1, 1, "scalar")
-        sort_pair(1, 2, "vector")
-        deal_codes(1)
-        deal_scales(1)
-        for t in (0, 1):
-            project(0, t)
-            real_part(0, t)
-        sort_pair(2, 0, "vector")
-        sort_pair(2, 2, "vector")
-        turn(1, 2)
-        turn(1, 3)
-        turn_out(1, 2, "vector")
-        turn_out(1, 3, "scalar")
         quantize_set(1)
-        sort_pair(3, 0, "vector")
-        project(0, 2)
-        real_part(0, 2)
-        turn(2, 0)
-        turn(2, 1)
-        project(0, 3)
-        real_part(0, 3)
-        turn_out(2, 1, "scalar")
-        turn_out(2, 0, "scalar")
-        turn(2, 2)
-        turn(2, 3)
-        sort_pair(3, 2, "vector")
-        turn_out(2, 3, "scalar")
-        turn_out(2, 2, "scalar")
-        project(1, 0)
-        add_imag(1, 0)
-        deal_codes(2)
-        project(1, 1)
-        add_imag(1, 1)
-        turn(3, 0)
-        turn(3, 1)
-        turn_out(3, 1, "scalar")
-        turn_out(3, 0, "scalar")
+        turn_pair(2, 0)
+        turn_pair(2, 2, "scalar", "vector")
+        deal_scales(1)
         quantize_set(2)
-        project(1, 2)
-        add_imag(1, 2)
-        turn(3, 2)
-        turn(3, 3)
-        turn_out(3, 3, "scalar")
-        turn_out(3, 2, "scalar")
-        project(1, 3)
-        add_imag(1, 3)
+        turn_pair(3, 0)
+        turn_pair(3, 2, "scalar", "scalar")
+        sort_pair(4, 0, "vector")
+        deal_codes(1)
+        real_pair(0, 0)
+        sort_pair(4, 2, "vector")
         quantize_set(3)
-
-        def real_step(c):
-            s = 2 * c + 2
-            turn(s, 0)
-            turn(s, 1)
-            interleave(c - 1, 0, 2)
-            if c > 1:
-                expand_out(c - 2, 3, 1, "vector")
-                expand_out(c - 2, 3, 0, "scalar")
-            turn_out(s, 1, "scalar")
-            turn_out(s, 0, "scalar")
-            sort_pair(s + 1, 0, "vector")
-            quantize_z(c - 1, 0, 2)
-            project(2 * c, 0)
-            real_part(2 * c, 0)
-            project(2 * c, 1)
-            real_part(2 * c, 1)
-            interleave(c - 1, 2, 4)
-            turn(s, 2)
-            turn(s, 3)
-            turn_out(s, 3, "scalar")
-            turn_out(s, 2, "scalar")
-            deal_scales(c + 1)
-            project(2 * c + 1, 0)
-            add_imag(2 * c + 1, 0)
-            project(2 * c + 1, 1)
-            add_imag(2 * c + 1, 1)
-            quantize_z(c - 1, 2, 4)
-            expand_half(c - 1, 0)
-            expand_out(c - 1, 0, 1, "scalar")
-            expand_out(c - 1, 0, 0, "scalar")
-
-        def imag_step(c):
-            s = 2 * c + 3
-            turn(s, 0)
-            turn(s, 1)
-            expand_out(c - 1, 1, 1, "vector")
-            expand_out(c - 1, 1, 0, "scalar")
-            turn_out(s, 1, "scalar")
-            turn_out(s, 0, "scalar")
-            if c == 1:
-                deal_codes(3)
-            quantize_set(s - 1)
-            project(2 * c, 2)
-            real_part(2 * c, 2)
-            project(2 * c + 1, 2)
-            add_imag(2 * c + 1, 2)
-            turn(s, 2)
-            turn(s, 3)
-            turn_out(s, 3, ("scalar", "vector")[c - 1])
-            turn_out(s, 2, "scalar")
-            project(2 * c, 3)
-            real_part(2 * c, 3)
-            project(2 * c + 1, 3)
-            add_imag(2 * c + 1, 3)
-            quantize_set(s)
-            expand_half(c - 1, 1)
-            expand_out(c - 1, 2, 1, "scalar")
-            expand_out(c - 1, 2, 0, "scalar")
-
-        for c in (1, 2):
-            real_step(c)
-            imag_step(c)
+        turn_pair(4, 0)
+        real_pair(0, 2)
+        turn_pair(4, 2)
+        deal_scales(2)
+        deal_codes(2)
+        imag_pair(1, 0)
+        sort_pair(5, 2, "scalar")
+        turn_pair(5, 0)
+        quantize_set(4)
+        imag_pair(1, 2)
+        turn_pair(5, 2)
+        sort_pair(6, 0, "vector")
+        interleave(0, 0, 2)
+        deal_scales(3)
+        quantize_z(0, 0, 2)
+        real_pair(2, 0)
+        turn_pair(6, 0)
+        interleave(0, 2, 4)
+        imag_pair(3, 0)
+        quantize_z(0, 2, 4)
+        expand_half(0, 0)
+        expand_out(0, 0, 1, "scalar")
+        expand_out(0, 0, 0, "scalar")
+        quantize_set(5)
+        turn_pair(6, 2)
+        expand_out(0, 1, 1, "vector")
+        expand_out(0, 1, 0, "scalar")
+        deal_codes(3)
+        project(2, 2)
+        real_part(2, 2)
+        project(3, 2)
+        add_imag(3, 2)
+        quantize_set(6)
+        turn_pair(7, 0)
+        project(2, 3)
+        real_part(2, 3)
+        project(3, 3)
+        add_imag(3, 3)
+        expand_half(0, 1)
+        expand_out(0, 2, 1, "scalar")
+        expand_out(0, 2, 0, "scalar")
+        interleave(1, 0, 2)
+        expand_out(0, 3, 1, "vector")
+        quantize_z(1, 0, 2)
+        expand_out(0, 3, 0, "scalar")
+        turn_pair(7, 2)
+        real_pair(4, 0)
+        interleave(1, 2, 4)
+        imag_pair(5, 0)
+        quantize_z(1, 2, 4)
+        expand_half(1, 0)
+        expand_out(1, 0, 1, "scalar")
+        expand_out(1, 0, 0, "scalar")
+        quantize_set(7)
+        expand_out(1, 1, 1, "vector")
+        expand_out(1, 1, 0, "scalar")
+        for t in (2, 3):
+            project(4, t)
+            real_part(4, t)
+            project(5, t)
+            add_imag(5, t)
+        expand_half(1, 1)
+        expand_out(1, 2, 1, "scalar")
+        expand_out(1, 2, 0, "scalar")
 
         expand_out(1, 3, 1, "scalar")
         expand_out(1, 3, 0, "scalar")

@@ -33,7 +33,7 @@ def tile_split_real_schrodinger_step_s14_kernel(tc, re, im, phase, v_words, v_sc
 
         v_raw = [keep.tile([P, 2, 1024], U8, name="v_raw%d" % c, align_bytes=256) for c in range(G)]
         v_dealt = [keep.tile([P, 2, 4, 256], U8, name="v_dealt%d" % c, align_bytes=256) for c in range(G)]
-        vs_raw = keep.tile([P, 2 * G, 512], U8, name="vs_raw", align_bytes=256)
+        vs_raw = [keep.tile([P, 2, 512], U8, name="vs_raw0", align_bytes=256), keep.tile([P, 6, 512], U8, name="vs_raw1", align_bytes=256)]
         vs_dealt = [keep.tile([P, 2, 4, 128], U8, name="vs_dealt%d" % c, align_bytes=256) for c in range(G)]
         u_codes = [keep.tile([P, 2048], U8, name="u_codes%d" % c, align_bytes=256) for c in range(G)]
         u_plane = keep.tile([P, G, 1024], U8, name="u_plane", align_bytes=256)
@@ -83,7 +83,8 @@ def tile_split_real_schrodinger_step_s14_kernel(tc, re, im, phase, v_words, v_sc
                 )
 
         nc.scalar.dma_start(out=theta[:], in_=phase.rearrange("c (p t) -> p c t", t=4))
-        nc.vector.memset(vs_raw[:].bitcast(I32), 0)
+        nc.vector.memset(vs_raw[0][:].bitcast(I32), 0)
+        nc.vector.memset(vs_raw[1][:].bitcast(I32), 0)
         make_identity(nc, ident[:])
         nc.vector.memset(u_plane[:].bitcast(I32), 0)
 
@@ -92,20 +93,22 @@ def tile_split_real_schrodinger_step_s14_kernel(tc, re, im, phase, v_words, v_sc
         load_x(0, 2, 4)
         load_set(1)
         load_v(0)
-        load_plane(vs_raw, v_scales)
+        load_plane(vs_raw[0], v_scales[0:2])
         load_set(2)
         load_set(3)
         load_v(1)
         load_set(4)
+        load_plane(vs_raw[1], v_scales[2:8])
         load_v(2)
         load_set(5)
-        load_v(3)
         load_set(6)
+        load_v(3)
         load_u(0)
         load_plane(u_plane, u_scales)
         load_set(7)
-        for c in range(1, G):
-            load_u(c)
+        load_u(1)
+        load_u(2)
+        load_u(3)
 
         theta_flat = theta[:].rearrange("p c t -> p (c t)")
 
@@ -194,7 +197,7 @@ def tile_split_real_schrodinger_step_s14_kernel(tc, re, im, phase, v_words, v_sc
             )
 
         def deal_scales(c):
-            raw = vs_raw[:, 2 * c : 2 * c + 2, :]
+            raw = vs_raw[0][:] if c == 0 else vs_raw[1][:, 2 * (c - 1) : 2 * c, :]
             nc.vector.tensor_copy(
                 out=vs_dealt[c][:].rearrange("p g t (b m) -> p g b t m", m=16),
                 in_=raw.rearrange("p g (b m t) -> p g b t m", t=4, m=16),
@@ -342,7 +345,6 @@ def tile_split_real_schrodinger_step_s14_kernel(tc, re, im, phase, v_words, v_sc
         quantize_set(1)
         turn_pair(2, 0)
         turn_pair(2, 2, "scalar", "vector")
-        deal_scales(1)
         quantize_set(2)
         turn_pair(3, 0)
         turn_pair(3, 2, "scalar", "scalar")
@@ -354,7 +356,7 @@ def tile_split_real_schrodinger_step_s14_kernel(tc, re, im, phase, v_words, v_sc
         turn_pair(4, 0)
         real_pair(0, 2)
         turn_pair(4, 2)
-        deal_scales(2)
+        deal_scales(1)
         deal_codes(2)
         imag_pair(1, 0)
         sort_pair(5, 2, "scalar")
@@ -364,12 +366,15 @@ def tile_split_real_schrodinger_step_s14_kernel(tc, re, im, phase, v_words, v_sc
         turn_pair(5, 2)
         sort_pair(6, 0, "vector")
         interleave(0, 0, 2)
-        deal_scales(3)
+        deal_scales(2)
         quantize_z(0, 0, 2)
         real_pair(2, 0)
         turn_pair(6, 0)
         interleave(0, 2, 4)
-        imag_pair(3, 0)
+        project(3, 0)
+        project(3, 1)
+        add_imag(3, 1)
+        add_imag(3, 0)
         quantize_z(0, 2, 4)
         expand_half(0, 0)
         expand_out(0, 0, 1, "scalar")
@@ -379,6 +384,7 @@ def tile_split_real_schrodinger_step_s14_kernel(tc, re, im, phase, v_words, v_sc
         expand_out(0, 1, 1, "vector")
         expand_out(0, 1, 0, "scalar")
         deal_codes(3)
+        deal_scales(3)
         project(2, 2)
         real_part(2, 2)
         project(3, 2)
@@ -421,10 +427,13 @@ def tile_split_real_schrodinger_step_s14_kernel(tc, re, im, phase, v_words, v_sc
         interleave(2, 0, 2)
         interleave(2, 2, 4)
         quantize_z(2, 0, 2)
-        for t in range(4):
+        for t in (0, 2):
             project(6, t)
+            project(6, t + 1)
+            real_part(6, t + 1)
             real_part(6, t)
             add_imag(6, t)
+            add_imag(6, t + 1)
             if t == 0:
                 quantize_z(2, 2, 4)
         expand_half(2, 0)

@@ -34,7 +34,7 @@ def tile_split_real_schrodinger_step_s14_kernel(tc, re, im, phase, v_words, v_sc
         v_raw = [keep.tile([P, 2, 1024], U8, name="v_raw%d" % c, align_bytes=256) for c in range(G)]
         v_dealt = [keep.tile([P, 2, 4, 256], U8, name="v_dealt%d" % c, align_bytes=256) for c in range(G)]
         vs_raw = [keep.tile([P, 2, 512], U8, name="vs_raw0", align_bytes=256), keep.tile([P, 6, 512], U8, name="vs_raw1", align_bytes=256)]
-        vs_dealt = [keep.tile([P, 2, 4, 128], U8, name="vs_dealt%d" % c, align_bytes=256) for c in range(G)]
+        vs_dealt = {c: keep.tile([P, 2, 4, 128], U8, name="vs_dealt%d" % c, align_bytes=256) for c in range(LAST)}
         u_codes = [keep.tile([P, 2048], U8, name="u_codes%d" % c, align_bytes=256) for c in range(G)]
         u_plane = keep.tile([P, G, 1024], U8, name="u_plane", align_bytes=256)
         ident = keep.tile([P, P], F32, name="ident")
@@ -57,7 +57,7 @@ def tile_split_real_schrodinger_step_s14_kernel(tc, re, im, phase, v_words, v_sc
 
         def load_x(s, q0, q1):
             part, i0 = tile_rows(s, q0)
-            xt = work.tile([P, q1 - q0, K], BF16, name="rows", bufs=24)
+            xt = keep.tile([P, q1 - q0, K], BF16, name="rows%d_%d" % (s, q0))
             rows = (re, im)[part][s // 2].rearrange("(p i) k -> p i k", i=4)
             nc.sync.dma_start(out=xt[:], in_=rows[:, i0 : i0 + q1 - q0, :])
             for q in range(q0, q1):
@@ -91,22 +91,23 @@ def tile_split_real_schrodinger_step_s14_kernel(tc, re, im, phase, v_words, v_sc
         load_x(0, 0, 1)
         load_x(0, 1, 2)
         load_x(0, 2, 4)
-        load_set(1)
+        for s in range(1, 4):
+            load_set(s)
         load_v(0)
         load_plane(vs_raw[0], v_scales[0:2])
-        load_set(2)
-        load_set(3)
-        load_v(1)
         load_set(4)
+        load_x(5, 0, 2)
+        load_x(5, 2, 3)
+        load_x(5, 3, 4)
         load_plane(vs_raw[1], v_scales[2:8])
-        load_v(2)
-        load_set(5)
+        load_v(1)
         load_set(6)
-        load_v(3)
         load_u(0)
         load_plane(u_plane, u_scales)
+        load_v(2)
         load_set(7)
         load_u(1)
+        load_v(3)
         load_u(2)
         load_u(3)
 
@@ -139,13 +140,15 @@ def tile_split_real_schrodinger_step_s14_kernel(tc, re, im, phase, v_words, v_sc
         def copy_on(engine, dst, src):
             if engine == "vector":
                 nc.vector.tensor_copy(out=dst, in_=src)
+            elif engine == "gpsimd":
+                nc.gpsimd.tensor_copy(out=dst, in_=src)
             else:
                 nc.scalar.copy(out=dst, in_=src)
 
         sorted_words = {}
 
-        def sort_pair(s, q, engine):
-            w = work.tile([P, 2, 512], F32, name="sorted_words", bufs=4)
+        def sort_pair(s, q, engine, slot):
+            w = work.tile([P, 2, 512], F32, name=slot, bufs=1, align_bytes=256)
             sorted_words[s, q] = w[:, 0, :]
             sorted_words[s, q + 1] = w[:, 1, :]
             copy_on(
@@ -171,17 +174,11 @@ def tile_split_real_schrodinger_step_s14_kernel(tc, re, im, phase, v_words, v_sc
 
         def turn_out(u, q, engine):
             if u not in grouped:
-                grouped[u] = work.tile([P, 2, 2048], BF16, name="grouped", bufs=2, align_bytes=256)
-                codes[u] = work.tile([P, 2, 512], U32, name="codes", bufs=6, align_bytes=256)
-                scales[u] = work.tile([P, 2, 512], U8, name="scales", bufs=6, align_bytes=256)
+                grouped[u] = work.tile([P, 2, 2048], BF16, name="grouped%d" % (2 if u == 7 else u % 2), bufs=1, align_bytes=256)
+                codes[u] = work.tile([P, 2, 512], U32, name="codes%d" % u, bufs=1, align_bytes=256)
+                scales[u] = keep.tile([P, 2, 512], U8, name="scales%d" % u, align_bytes=256)
             dst = grouped[u][:].bitcast(F32).rearrange("p g (n e) -> p g n e", e=2)[:, :, 128 * q : 128 * (q + 1), :]
             copy_on(engine, dst, banks["T", u, q][:].rearrange("p (g e r) -> p g r e", g=2, e=2))
-
-        def quantize_x(u, g, q0=0, q1=4):
-            cols = slice(128 * q0, 128 * q1)
-            nc.vector.quantize_mx(
-                out=codes[u][:, g, cols].bitcast(FP8X4), scales=scales[u][:, g, cols], in_=grouped[u][:, g, 512 * q0 : 512 * q1]
-            )
 
         def quantize_set(s):
             nc.vector.quantize_mx(
@@ -190,17 +187,21 @@ def tile_split_real_schrodinger_step_s14_kernel(tc, re, im, phase, v_words, v_sc
                 in_=grouped[s][:].rearrange("p g n -> p (g n)"),
             )
 
-        def deal_codes(c):
-            nc.vector.tensor_copy(
-                out=v_dealt[c][:].bitcast(U16).rearrange("p g t (b m) -> p g b t m", m=8),
-                in_=v_raw[c][:].bitcast(U16).rearrange("p g (b m t) -> p g b t m", t=4, m=8),
+        def deal_codes(c, engine="vector", g0=0, g1=2):
+            copy_on(
+                engine,
+                v_dealt[c][:, g0:g1].bitcast(U16).rearrange("p g t (b m) -> p g b t m", m=8),
+                v_raw[c][:, g0:g1].bitcast(U16).rearrange("p g (b m t) -> p g b t m", t=4, m=8),
             )
 
-        def deal_scales(c):
+        def deal_scales(c, engine="vector", g0=0, g1=2):
+            if c not in vs_dealt:
+                vs_dealt[c] = work.tile([P, 2, 4, 128], U8, name="stage_d", bufs=1, align_bytes=256)
             raw = vs_raw[0][:] if c == 0 else vs_raw[1][:, 2 * (c - 1) : 2 * c, :]
-            nc.vector.tensor_copy(
-                out=vs_dealt[c][:].rearrange("p g t (b m) -> p g b t m", m=16),
-                in_=raw.rearrange("p g (b m t) -> p g b t m", t=4, m=16),
+            copy_on(
+                engine,
+                vs_dealt[c][:, g0:g1].rearrange("p g t (b m) -> p g b t m", m=16),
+                raw[:, g0:g1].rearrange("p g (b m t) -> p g b t m", t=4, m=16),
             )
 
         def project(u, t):
@@ -217,6 +218,31 @@ def tile_split_real_schrodinger_step_s14_kernel(tc, re, im, phase, v_words, v_sc
                     stop=(g == 1),
                 )
 
+        halves = {}
+
+        def project_half(u, t, part, beside=None):
+            c = u // 2
+            cols = slice(256 * part, 256 * (part + 1))
+            if beside is None:
+                halves[u, t, part] = new_bank(("AB", u, t, part))[:, 0:256]
+            else:
+                halves[u, t, part] = banks["AB", u, beside, part][:, 256:512]
+            for g in range(2):
+                nc.tensor.matmul_mx(
+                    out=halves[u, t, part],
+                    lhsT=v_dealt[c][:, g, t, :].bitcast(FP4X4),
+                    lhsT_scale=vs_dealt[c][:, g, t, :],
+                    rhs=codes[u][:, g, cols].bitcast(FP8X4),
+                    rhs_scale=scales[u][:, g, cols],
+                    start=(g == 0),
+                    stop=(g == 1),
+                )
+
+        def amplitudes(s, t, part, cols):
+            if (s, t, part) in halves:
+                return halves[s, t, part]
+            return banks["AB", s, t][:, cols]
+
         a_cos = {}
         z_rows = {}
         z_grouped = {}
@@ -231,15 +257,15 @@ def tile_split_real_schrodinger_step_s14_kernel(tc, re, im, phase, v_words, v_sc
         def real_part(s, t, engine="scalar"):
             c = s // 2
             if (c, t) not in a_cos:
-                a_cos[c, t] = work.tile([P, 512], F32, name="a_cos", bufs=5)
+                a_cos[c, t] = work.tile([P, 512], F32, name="a_cos", bufs=6)
             a_cols, b_cols, cols = amplitude_cols(s)
             if engine == "vector":
                 nc.vector.tensor_scalar(
-                    out=a_cos[c, t][:, cols], in0=banks["AB", s, t][:, a_cols], scalar1=trig[:, 1, 4 * c + t : 4 * c + t + 1], scalar2=None, op0=ALU.mult
+                    out=a_cos[c, t][:, cols], in0=amplitudes(s, t, 0, a_cols), scalar1=trig[:, 1, 4 * c + t : 4 * c + t + 1], scalar2=None, op0=ALU.mult
                 )
             else:
                 nc.scalar.activation(
-                    out=a_cos[c, t][:, cols], in_=banks["AB", s, t][:, a_cols], func=ACT.Copy, scale=trig[:, 1, 4 * c + t : 4 * c + t + 1]
+                    out=a_cos[c, t][:, cols], in_=amplitudes(s, t, 0, a_cols), func=ACT.Copy, scale=trig[:, 1, 4 * c + t : 4 * c + t + 1]
                 )
 
         def add_imag(s, t):
@@ -250,13 +276,13 @@ def tile_split_real_schrodinger_step_s14_kernel(tc, re, im, phase, v_words, v_sc
                 z_scales[c] = work.tile([P, 512], U8, name="z_scales", bufs=2, align_bytes=256)
             a_cols, b_cols, cols = amplitude_cols(s)
             nc.vector.scalar_tensor_tensor(
-                out=z_rows[c][:, t, cols], in0=banks["AB", s, t][:, b_cols], scalar=trig[:, 0, 4 * c + t : 4 * c + t + 1],
+                out=z_rows[c][:, t, cols], in0=amplitudes(s, t, 1, b_cols), scalar=trig[:, 0, 4 * c + t : 4 * c + t + 1],
                 in1=a_cos[c, t][:, cols], op0=ALU.mult, op1=ALU.add,
             )
 
-        def interleave(c, i0, i1, engine="vector"):
+        def interleave(c, i0, i1, slot, engine="vector"):
             cols = slice(128 * i0, 128 * i1)
-            zt = work.tile([P, 128 * (i1 - i0), 4], BF16, name="z_grouped", bufs=3, align_bytes=256)
+            zt = work.tile([P, 128 * (i1 - i0), 4], BF16, name=slot, bufs=1, align_bytes=256)
             z_grouped[c, i0] = zt
             copy_on(
                 engine,
@@ -284,17 +310,13 @@ def tile_split_real_schrodinger_step_s14_kernel(tc, re, im, phase, v_words, v_sc
                 stop=True,
             )
 
-        def expand_half(c, h):
-            for i in (2 * h, 2 * h + 1):
-                for n in range(2):
-                    expand(c, i, n)
-
         out_rows = {}
+        out_slots = ["out%d" % j for j in range(5)] + ["codes%d" % j for j in range(6)] + ["grouped0", "grouped2", "grouped1", "codes6", "stage_e"]
         copied = []
 
         def expand_out(c, i, n, engine):
             if (c, i) not in out_rows:
-                out_rows[c, i] = work.tile([P, 1024], F32, name="rows", bufs=24)
+                out_rows[c, i] = work.tile([P, 1024], F32, name=out_slots[4 * c + i], bufs=1, align_bytes=256)
             cols = slice(512 * n, 512 * (n + 1))
             copy_on(engine, out_rows[c, i][:, cols], banks["O", c, i, n][:])
             copied.append((c, i, n))
@@ -304,175 +326,193 @@ def tile_split_real_schrodinger_step_s14_kernel(tc, re, im, phase, v_words, v_sc
             elif (c, i, 1 - n) in copied:
                 nc.sync.dma_start(out=dst, in_=out_rows[c, i][:])
 
-        def row_out(c, i, engine):
-            expand_out(c, i, 0, engine)
-            expand_out(c, i, 1, engine)
+        S, V = "scalar", "vector"
 
-        def turn_set(s):
-            for q in range(4):
-                turn(s, q)
-
-        def turn_pair(s, q, first="scalar", second="scalar"):
+        def turn_pair(s, q, first=S, second=S):
             turn(s, q)
             turn(s, q + 1)
             turn_out(s, q + 1, first)
             turn_out(s, q, second)
 
-        def real_pair(s, t):
-            project(s, t)
-            project(s, t + 1)
-            real_part(s, t)
-            real_part(s, t + 1)
+        def expand_row(c, i, first=S, second=S):
+            expand(c, i, 0)
+            expand(c, i, 1)
+            expand_out(c, i, 1, first)
+            expand_out(c, i, 0, second)
 
-        def imag_pair(s, t):
-            for j in range(2):
-                project(s, t + j)
-                add_imag(s, t + j)
+        def imag_modes(c, t):
+            project(2 * c + 1, t)
 
+        def expand_pe(c, i):
+            expand(c, i, 0)
+            expand(c, i, 1)
+
+        def both_out(c, i):
+            expand_out(c, i, 1, S)
+            expand_out(c, i, 0, S)
+
+        def a_step(c, t):
+            project(2 * c, t)
+            real_part(2 * c, t)
+
+        def turn_pe(s, q):
+            turn(s, q)
+            turn(s, q + 1)
+
+        def turn_both(s, q, first=S, second=S):
+            turn_out(s, q + 1, first)
+            turn_out(s, q, second)
+
+        G_ = "gpsimd"
         trig_reduce()
         turn(0, 0)
-        turn_out(0, 0, "scalar")
+        turn_out(0, 0, S)
         trig_square()
         turn(0, 1)
-        turn_out(0, 1, "vector")
+        turn_out(0, 1, V)
         trig_finish()
-        turn_pair(0, 2, "scalar", "vector")
-        quantize_set(0)
-        turn_pair(1, 0)
-        deal_codes(0)
-        turn_pair(1, 2, "scalar", "scalar")
-        deal_scales(0)
-        quantize_set(1)
-        turn_pair(2, 0)
-        turn_pair(2, 2, "scalar", "vector")
-        quantize_set(2)
-        turn_pair(3, 0)
-        turn_pair(3, 2, "scalar", "scalar")
-        sort_pair(4, 0, "vector")
-        deal_codes(1)
-        real_pair(0, 0)
-        sort_pair(4, 2, "vector")
-        quantize_set(3)
-        turn_pair(4, 0)
-        real_pair(0, 2)
-        turn_pair(4, 2)
-        deal_scales(1)
-        deal_codes(2)
-        imag_pair(1, 0)
-        sort_pair(5, 2, "scalar")
+        turn_pair(0, 2, S, V)
+        for s in range(1, 5):
+            turn_pair(s, 0)
+            quantize_set(s - 1)
+            if s == 4:
+                deal_codes(0)
+                deal_scales(0)
+            turn_pair(s, 2, S, V)
         turn_pair(5, 0)
         quantize_set(4)
-        imag_pair(1, 2)
-        turn_pair(5, 2)
-        sort_pair(6, 0, "vector")
-        interleave(0, 0, 2)
+        turn(5, 2)
+        turn_out(5, 2, S)
+        turn(5, 3)
+        turn_out(5, 3, S)
+
+        a_step(0, 0)
+        deal_scales(1)
+        imag_modes(0, 0)
+        deal_codes(1, S)
         deal_scales(2)
+        quantize_set(5)
+        sort_pair(6, 0, G_, "grouped1")
+        sort_pair(6, 2, G_, "stage_c")
+        add_imag(1, 0)
+        a_step(0, 1)
+        imag_modes(0, 1)
+        add_imag(1, 1)
+        a_step(0, 2)
+        a_step(0, 3)
+        imag_modes(0, 2)
+        add_imag(1, 2)
+        imag_modes(0, 3)
+        add_imag(1, 3)
+
+        interleave(0, 0, 2, "stage_a")
+        a_step(1, 0)
+        deal_codes(2, S)
+        interleave(0, 2, 4, "stage_b")
         quantize_z(0, 0, 2)
-        real_pair(2, 0)
-        turn_pair(6, 0)
-        interleave(0, 2, 4)
-        project(3, 0)
-        project(3, 1)
-        add_imag(3, 1)
+        imag_modes(1, 0)
         add_imag(3, 0)
         quantize_z(0, 2, 4)
-        expand_half(0, 0)
-        expand_out(0, 0, 1, "scalar")
-        expand_out(0, 0, 0, "scalar")
-        quantize_set(5)
-        turn_pair(6, 2)
-        expand_out(0, 1, 1, "vector")
-        expand_out(0, 1, 0, "scalar")
-        deal_codes(3)
-        deal_scales(3)
-        project(2, 2)
-        real_part(2, 2)
-        project(3, 2)
+        sort_pair(7, 0, G_, "stage_b")
+        sort_pair(7, 2, G_, "stage_e")
+        deal_codes(3, G_)
+        turn_pe(6, 0)
+        a_step(1, 1)
+        turn_both(6, 0, S, S)
+        imag_modes(1, 1)
+        add_imag(3, 1)
+        expand_pe(0, 0)
+        expand_out(0, 0, 1, V)
+        expand_out(0, 0, 0, V)
+        turn_pe(6, 2)
+        turn_both(6, 2)
+        expand_pe(0, 1)
+        expand_out(0, 1, 0, V)
+        a_step(1, 2)
+        expand_out(0, 1, 1, V)
+        a_step(1, 3)
+        imag_modes(1, 2)
         add_imag(3, 2)
-        quantize_set(6)
-        turn_pair(7, 0)
-        project(2, 3)
-        real_part(2, 3)
-        project(3, 3)
+        expand_pe(0, 2)
+        both_out(0, 2)
+        imag_modes(1, 3)
         add_imag(3, 3)
-        expand_half(0, 1)
-        expand_out(0, 2, 1, "scalar")
-        expand_out(0, 2, 0, "scalar")
-        interleave(1, 0, 2)
-        expand_out(0, 3, 1, "vector")
-        quantize_z(1, 0, 2)
-        expand_out(0, 3, 0, "scalar")
-        turn_pair(7, 2)
-        real_pair(4, 0)
-        interleave(1, 2, 4)
-        imag_pair(5, 0)
-        quantize_z(1, 2, 4)
-        expand_half(1, 0)
-        expand_out(1, 0, 1, "scalar")
-        expand_out(1, 0, 0, "scalar")
-        quantize_set(7)
-        expand_out(1, 1, 1, "vector")
-        expand_out(1, 1, 0, "scalar")
-        for t in (2, 3):
-            project(4, t)
-            real_part(4, t)
-            project(5, t)
-            add_imag(5, t)
-        expand_half(1, 1)
-        expand_out(1, 2, 1, "scalar")
-        expand_out(1, 2, 0, "scalar")
 
-        expand_out(1, 3, 1, "scalar")
-        expand_out(1, 3, 0, "scalar")
-        interleave(2, 0, 2)
-        interleave(2, 2, 4)
+        expand_pe(0, 3)
+        interleave(1, 0, 2, "stage_a")
+        both_out(0, 3)
+        a_step(2, 0)
+        interleave(1, 2, 4, "stage_d")
+        quantize_z(1, 0, 2)
+        imag_modes(2, 0)
+        add_imag(5, 0)
+        quantize_set(6)
+        quantize_z(1, 2, 4)
+        deal_scales(3, G_)
+        turn_pe(7, 0)
+        turn_both(7, 0)
+        a_step(2, 1)
+        expand_pe(1, 0)
+        expand_out(1, 0, 1, S)
+        imag_modes(2, 1)
+        add_imag(5, 1)
+        expand_out(1, 0, 0, V)
+        turn_pe(7, 2)
+        turn_both(7, 2, S, V)
+        expand_pe(1, 1)
+        quantize_set(7)
+        expand_out(1, 1, 0, S)
+        a_step(2, 2)
+        expand_out(1, 1, 1, S)
+        a_step(2, 3)
+        imag_modes(2, 2)
+        add_imag(5, 2)
+        expand_pe(1, 2)
+        both_out(1, 2)
+        imag_modes(2, 3)
+        add_imag(5, 3)
+
+        expand_pe(1, 3)
+        interleave(2, 0, 2, "stage_a")
+        interleave(2, 2, 4, "stage_b")
+        both_out(1, 3)
         quantize_z(2, 0, 2)
-        for t in (0, 2):
+        quantize_z(2, 2, 4)
+        for t in range(4):
             project(6, t)
-            project(6, t + 1)
-            real_part(6, t + 1)
             real_part(6, t)
             add_imag(6, t)
-            add_imag(6, t + 1)
-            if t == 0:
-                quantize_z(2, 2, 4)
-        expand_half(2, 0)
-        expand_out(2, 0, 1, "scalar")
-        expand_out(2, 0, 0, "scalar")
-        expand_out(2, 1, 1, "vector")
-        expand_out(2, 1, 0, "vector")
-        interleave(LAST, 0, 2)
-        project(7, 0)
+        interleave(LAST, 0, 2, "stage_a", G_)
+        expand_pe(2, 0)
+        both_out(2, 0)
+        expand_pe(2, 1)
+        expand_out(2, 1, 1, V)
+        expand_out(2, 1, 0, V)
+        project_half(7, 0, 0)
+        project_half(7, 1, 0, 0)
         real_part(7, 0)
-        add_imag(7, 0)
-        quantize_z(LAST, 0, 2)
-        expand(2, 2, 0)
-        expand(2, 2, 1)
-        expand_out(2, 2, 1, "scalar")
-        expand_out(2, 2, 0, "scalar")
-        project(7, 1)
         real_part(7, 1)
-        add_imag(7, 1)
-        expand(2, 3, 0)
-        expand(2, 3, 1)
-        expand_out(2, 3, 1, "vector")
-        expand_out(2, 3, 0, "scalar")
-        project(7, 2)
+        expand_pe(2, 2)
+        expand_out(2, 2, 1, S)
+        expand_out(2, 2, 0, V)
+        quantize_z(LAST, 0, 2)
+        project_half(7, 2, 0)
+        project_half(7, 3, 0, 2)
         real_part(7, 2)
-        add_imag(7, 2)
-        project(7, 3)
         real_part(7, 3)
-        add_imag(7, 3)
-        expand_half(LAST, 0)
-        expand_out(LAST, 0, 1, "scalar")
-        expand_out(LAST, 0, 0, "scalar")
-        interleave(LAST, 2, 3)
-        interleave(LAST, 3, 4)
+        expand_pe(2, 3)
+        both_out(2, 3)
+        for t in range(4):
+            project_half(7, t, 1)
+            add_imag(7, t)
+
+        expand_row(LAST, 0)
+        expand_row(LAST, 1)
+        interleave(LAST, 2, 3, "stage_b")
+        interleave(LAST, 3, 4, "stage_c")
         quantize_z(LAST, 2, 3)
         quantize_z(LAST, 3, 4)
-        expand_out(LAST, 1, 1, "scalar")
-        expand_out(LAST, 1, 0, "scalar")
         for i in (2, 3):
             for n in range(2):
                 expand(LAST, i, n)
-                expand_out(LAST, i, n, ("vector", "scalar")[n])
+                expand_out(LAST, i, n, (V, S)[n])

@@ -188,20 +188,22 @@ def tile_split_real_schrodinger_step_s14_kernel(tc, re, im, phase, v_words, v_sc
             )
 
         def deal_codes(c, engine="vector", g0=0, g1=2):
+            run = P if engine == "gpsimd" else 8
             copy_on(
                 engine,
-                v_dealt[c][:, g0:g1].bitcast(U16).rearrange("p g t (b m) -> p g b t m", m=8),
-                v_raw[c][:, g0:g1].bitcast(U16).rearrange("p g (b m t) -> p g b t m", t=4, m=8),
+                v_dealt[c][:, g0:g1].bitcast(U16).rearrange("p g t (b m) -> p g b t m", m=run),
+                v_raw[c][:, g0:g1].bitcast(U16).rearrange("p g (b m t) -> p g b t m", t=4, m=run),
             )
 
         def deal_scales(c, engine="vector", g0=0, g1=2):
             if c not in vs_dealt:
                 vs_dealt[c] = work.tile([P, 2, 4, 128], U8, name="stage_d", bufs=1, align_bytes=256)
             raw = vs_raw[0][:] if c == 0 else vs_raw[1][:, 2 * (c - 1) : 2 * c, :]
+            run = P if engine == "gpsimd" else 16
             copy_on(
                 engine,
-                vs_dealt[c][:, g0:g1].rearrange("p g t (b m) -> p g b t m", m=16),
-                raw[:, g0:g1].rearrange("p g (b m t) -> p g b t m", t=4, m=16),
+                vs_dealt[c][:, g0:g1].rearrange("p g t (b m) -> p g b t m", m=run),
+                raw[:, g0:g1].rearrange("p g (b m t) -> p g b t m", t=4, m=run),
             )
 
         def project(u, t):
@@ -284,10 +286,11 @@ def tile_split_real_schrodinger_step_s14_kernel(tc, re, im, phase, v_words, v_sc
             cols = slice(128 * i0, 128 * i1)
             zt = work.tile([P, 128 * (i1 - i0), 4], BF16, name=slot, bufs=1, align_bytes=256)
             z_grouped[c, i0] = zt
+            run = 1 if engine == "gpsimd" else 4
             copy_on(
                 engine,
-                zt[:].rearrange("p (b n) t -> p b t n", n=4),
-                z_rows[c][:, :, cols].rearrange("p t (b n) -> p b t n", n=4),
+                zt[:].rearrange("p (b n) t -> p b t n", n=run),
+                z_rows[c][:, :, cols].rearrange("p t (b n) -> p b t n", n=run),
             )
 
         def quantize_z(c, i0, i1):

@@ -34,7 +34,7 @@ def tile_split_real_schrodinger_step_s14_kernel(tc, re, im, phase, v_words, v_sc
         v_raw = [keep.tile([P, 2, 1024], U8, name="v_raw%d" % c, align_bytes=256) for c in range(G)]
         v_dealt = [keep.tile([P, 2, 4, 256], U8, name="v_dealt%d" % c, align_bytes=256) for c in range(G)]
         vs_raw = [keep.tile([P, 2, 512], U8, name="vs_raw0", align_bytes=256), keep.tile([P, 6, 512], U8, name="vs_raw1", align_bytes=256)]
-        vs_dealt = {c: keep.tile([P, 2, 4, 128], U8, name="vs_dealt%d" % c, align_bytes=256) for c in range(LAST)}
+        vs_dealt = [keep.tile([P, 2, 4, 128], U8, name="vs_dealt%d" % c, align_bytes=256) for c in range(G)]
         u_codes = [keep.tile([P, 2048], U8, name="u_codes%d" % c, align_bytes=256) for c in range(G)]
         u_plane = keep.tile([P, G, 1024], U8, name="u_plane", align_bytes=256)
         ident = keep.tile([P, P], F32, name="ident")
@@ -57,7 +57,7 @@ def tile_split_real_schrodinger_step_s14_kernel(tc, re, im, phase, v_words, v_sc
 
         def load_x(s, q0, q1):
             part, i0 = tile_rows(s, q0)
-            xt = keep.tile([P, q1 - q0, K], BF16, name="rows%d_%d" % (s, q0))
+            xt = keep.tile([P, q1 - q0, K], BF16, name="rows%d_%d" % (s, q0), align_bytes=256)
             rows = (re, im)[part][s // 2].rearrange("(p i) k -> p i k", i=4)
             nc.sync.dma_start(out=xt[:], in_=rows[:, i0 : i0 + q1 - q0, :])
             for q in range(q0, q1):
@@ -91,22 +91,22 @@ def tile_split_real_schrodinger_step_s14_kernel(tc, re, im, phase, v_words, v_sc
         load_x(0, 0, 1)
         load_x(0, 1, 2)
         load_x(0, 2, 4)
-        for s in range(1, 4):
-            load_set(s)
-        load_v(0)
+        load_x(1, 0, 2)
         load_plane(vs_raw[0], v_scales[0:2])
-        load_set(4)
-        load_x(5, 0, 2)
-        load_x(5, 2, 3)
-        load_x(5, 3, 4)
-        load_plane(vs_raw[1], v_scales[2:8])
+        load_v(0)
+        load_x(1, 2, 4)
+        load_set(2)
+        load_set(3)
         load_v(1)
-        load_set(6)
+        load_plane(vs_raw[1], v_scales[2:8])
+        load_set(4)
         load_u(0)
         load_plane(u_plane, u_scales)
+        load_set(5)
         load_v(2)
-        load_set(7)
+        load_set(6)
         load_u(1)
+        load_set(7)
         load_v(3)
         load_u(2)
         load_u(3)
@@ -174,7 +174,7 @@ def tile_split_real_schrodinger_step_s14_kernel(tc, re, im, phase, v_words, v_sc
 
         def turn_out(u, q, engine):
             if u not in grouped:
-                grouped[u] = work.tile([P, 2, 2048], BF16, name="grouped%d" % (2 if u == 7 else u % 2), bufs=1, align_bytes=256)
+                grouped[u] = work.tile([P, 2, 2048], BF16, name="grouped%d" % (u % 2), bufs=1, align_bytes=256)
                 codes[u] = work.tile([P, 2, 512], U32, name="codes%d" % u, bufs=1, align_bytes=256)
                 scales[u] = keep.tile([P, 2, 512], U8, name="scales%d" % u, align_bytes=256)
             dst = grouped[u][:].bitcast(F32).rearrange("p g (n e) -> p g n e", e=2)[:, :, 128 * q : 128 * (q + 1), :]
@@ -188,22 +188,18 @@ def tile_split_real_schrodinger_step_s14_kernel(tc, re, im, phase, v_words, v_sc
             )
 
         def deal_codes(c, engine="vector", g0=0, g1=2):
-            run = P if engine == "gpsimd" else 8
             copy_on(
                 engine,
-                v_dealt[c][:, g0:g1].bitcast(U16).rearrange("p g t (b m) -> p g b t m", m=run),
-                v_raw[c][:, g0:g1].bitcast(U16).rearrange("p g (b m t) -> p g b t m", t=4, m=run),
+                v_dealt[c][:, g0:g1].bitcast(U16).rearrange("p g t (b m) -> p g b t m", m=8),
+                v_raw[c][:, g0:g1].bitcast(U16).rearrange("p g (b m t) -> p g b t m", t=4, m=8),
             )
 
         def deal_scales(c, engine="vector", g0=0, g1=2):
-            if c not in vs_dealt:
-                vs_dealt[c] = work.tile([P, 2, 4, 128], U8, name="stage_d", bufs=1, align_bytes=256)
             raw = vs_raw[0][:] if c == 0 else vs_raw[1][:, 2 * (c - 1) : 2 * c, :]
-            run = P if engine == "gpsimd" else 16
             copy_on(
                 engine,
-                vs_dealt[c][:, g0:g1].rearrange("p g t (b m) -> p g b t m", m=run),
-                raw[:, g0:g1].rearrange("p g (b m t) -> p g b t m", t=4, m=run),
+                vs_dealt[c][:, g0:g1].rearrange("p g t (b m) -> p g b t m", m=16),
+                raw[:, g0:g1].rearrange("p g (b m t) -> p g b t m", t=4, m=16),
             )
 
         def project(u, t):
@@ -286,11 +282,10 @@ def tile_split_real_schrodinger_step_s14_kernel(tc, re, im, phase, v_words, v_sc
             cols = slice(128 * i0, 128 * i1)
             zt = work.tile([P, 128 * (i1 - i0), 4], BF16, name=slot, bufs=1, align_bytes=256)
             z_grouped[c, i0] = zt
-            run = 1 if engine == "gpsimd" else 4
             copy_on(
                 engine,
-                zt[:].rearrange("p (b n) t -> p b t n", n=run),
-                z_rows[c][:, :, cols].rearrange("p t (b n) -> p b t n", n=run),
+                zt[:].rearrange("p (b n) t -> p b t n", n=4),
+                z_rows[c][:, :, cols].rearrange("p t (b n) -> p b t n", n=4),
             )
 
         def quantize_z(c, i0, i1):
@@ -314,7 +309,7 @@ def tile_split_real_schrodinger_step_s14_kernel(tc, re, im, phase, v_words, v_sc
             )
 
         out_rows = {}
-        out_slots = ["out%d" % j for j in range(5)] + ["codes%d" % j for j in range(6)] + ["grouped0", "grouped2", "grouped1", "codes6", "stage_e"]
+        out_slots = ["out%d" % j for j in range(4)] + ["codes%d" % j for j in range(6)] + ["sorted%d" % j for j in range(4)] + ["grouped0", "grouped1"]
         copied = []
 
         def expand_out(c, i, n, engine):
@@ -343,6 +338,9 @@ def tile_split_real_schrodinger_step_s14_kernel(tc, re, im, phase, v_words, v_sc
             expand_out(c, i, 1, first)
             expand_out(c, i, 0, second)
 
+        def real_modes(c, t):
+            project(2 * c, t)
+
         def imag_modes(c, t):
             project(2 * c + 1, t)
 
@@ -354,143 +352,113 @@ def tile_split_real_schrodinger_step_s14_kernel(tc, re, im, phase, v_words, v_sc
             expand_out(c, i, 1, S)
             expand_out(c, i, 0, S)
 
-        def a_step(c, t):
-            project(2 * c, t)
-            real_part(2 * c, t)
-
-        def turn_pe(s, q):
-            turn(s, q)
-            turn(s, q + 1)
-
-        def turn_both(s, q, first=S, second=S):
-            turn_out(s, q + 1, first)
-            turn_out(s, q, second)
-
-        G_ = "gpsimd"
         trig_reduce()
         turn(0, 0)
         turn_out(0, 0, S)
         trig_square()
         turn(0, 1)
-        turn_out(0, 1, V)
+        turn_out(0, 1, S)
         trig_finish()
         turn_pair(0, 2, S, V)
-        for s in range(1, 5):
-            turn_pair(s, 0)
-            quantize_set(s - 1)
-            if s == 4:
-                deal_codes(0)
-                deal_scales(0)
-            turn_pair(s, 2, S, V)
-        turn_pair(5, 0)
-        quantize_set(4)
-        turn(5, 2)
-        turn_out(5, 2, S)
-        turn(5, 3)
-        turn_out(5, 3, S)
+        deal_scales(0)
+        quantize_set(0)
+        deal_codes(0)
+        turn_pair(1, 0)
+        turn_pair(1, 2)
+        sort_pair(2, 0, V, "sorted0")
 
-        a_step(0, 0)
+        real_modes(0, 0)
+        real_modes(0, 1)
+        sort_pair(2, 2, V, "sorted1")
+        quantize_set(1)
+        real_part(0, 0)
+        real_part(0, 1)
+        turn_pair(2, 0)
+        sort_pair(3, 0, V, "sorted2")
+        real_modes(0, 2)
+        real_modes(0, 3)
+        real_part(0, 3)
+        real_part(0, 2)
+        sort_pair(3, 2, V, "sorted3")
+        turn_pair(2, 2)
+        deal_codes(1)
         deal_scales(1)
         imag_modes(0, 0)
-        deal_codes(1, S)
-        deal_scales(2)
-        quantize_set(5)
-        sort_pair(6, 0, G_, "grouped1")
-        sort_pair(6, 2, G_, "stage_c")
-        add_imag(1, 0)
-        a_step(0, 1)
         imag_modes(0, 1)
+        add_imag(1, 0)
+        quantize_set(2)
         add_imag(1, 1)
-        a_step(0, 2)
-        a_step(0, 3)
+        turn_pair(3, 0)
         imag_modes(0, 2)
         add_imag(1, 2)
         imag_modes(0, 3)
         add_imag(1, 3)
+        turn_pair(3, 2)
 
-        interleave(0, 0, 2, "stage_a")
-        a_step(1, 0)
-        deal_codes(2, S)
-        interleave(0, 2, 4, "stage_b")
-        quantize_z(0, 0, 2)
-        imag_modes(1, 0)
-        add_imag(3, 0)
-        quantize_z(0, 2, 4)
-        sort_pair(7, 0, G_, "stage_b")
-        sort_pair(7, 2, G_, "stage_e")
-        deal_codes(3, G_)
-        turn_pe(6, 0)
-        a_step(1, 1)
-        turn_both(6, 0, S, S)
-        imag_modes(1, 1)
-        add_imag(3, 1)
-        expand_pe(0, 0)
-        expand_out(0, 0, 1, V)
-        expand_out(0, 0, 0, V)
-        turn_pe(6, 2)
-        turn_both(6, 2)
-        expand_pe(0, 1)
-        expand_out(0, 1, 0, V)
-        a_step(1, 2)
-        expand_out(0, 1, 1, V)
-        a_step(1, 3)
-        imag_modes(1, 2)
-        add_imag(3, 2)
-        expand_pe(0, 2)
-        both_out(0, 2)
-        imag_modes(1, 3)
-        add_imag(3, 3)
+        for c in (1, 2):
+            p = c - 1
+            interleave(p, 0, 2, "stage_a")
+            interleave(p, 2, 4, "stage_b")
+            quantize_z(p, 0, 2)
+            real_modes(c, 0)
+            real_modes(c, 1)
+            real_part(2 * c, 1)
+            real_part(2 * c, 0)
+            quantize_set(2 * c + 1)
+            quantize_z(p, 2, 4)
+            turn_pair(2 * c + 2, 0)
+            if c == 1:
+                sort_pair(5, 0, V, "sorted0")
+            real_modes(c, 2)
+            real_modes(c, 3)
+            real_part(2 * c, 3)
+            real_part(2 * c, 2)
+            expand_pe(p, 0)
+            expand_out(p, 0, 1, V)
+            expand_out(p, 0, 0, V)
+            deal_codes(c + 1)
+            turn_pair(2 * c + 2, 2)
+            expand_pe(p, 1)
+            both_out(p, 1)
+            imag_modes(c, 0)
+            imag_modes(c, 1)
+            deal_scales(c + 1)
+            add_imag(2 * c + 1, 1)
+            add_imag(2 * c + 1, 0)
+            quantize_set(2 * c + 2)
+            turn_pair(2 * c + 3, 0)
+            imag_modes(c, 2)
+            add_imag(2 * c + 1, 2)
+            expand_pe(p, 2)
+            both_out(p, 2)
+            imag_modes(c, 3)
+            add_imag(2 * c + 1, 3)
+            expand_pe(p, 3)
+            both_out(p, 3)
+            turn_pair(2 * c + 3, 2)
 
-        expand_pe(0, 3)
-        interleave(1, 0, 2, "stage_a")
-        both_out(0, 3)
-        a_step(2, 0)
-        interleave(1, 2, 4, "stage_d")
-        quantize_z(1, 0, 2)
-        imag_modes(2, 0)
-        add_imag(5, 0)
-        quantize_set(6)
-        quantize_z(1, 2, 4)
-        deal_scales(3, G_)
-        turn_pe(7, 0)
-        turn_both(7, 0)
-        a_step(2, 1)
-        expand_pe(1, 0)
-        expand_out(1, 0, 1, S)
-        imag_modes(2, 1)
-        add_imag(5, 1)
-        expand_out(1, 0, 0, V)
-        turn_pe(7, 2)
-        turn_both(7, 2, S, V)
-        expand_pe(1, 1)
-        quantize_set(7)
-        expand_out(1, 1, 0, S)
-        a_step(2, 2)
-        expand_out(1, 1, 1, S)
-        a_step(2, 3)
-        imag_modes(2, 2)
-        add_imag(5, 2)
-        expand_pe(1, 2)
-        both_out(1, 2)
-        imag_modes(2, 3)
-        add_imag(5, 3)
-
-        expand_pe(1, 3)
         interleave(2, 0, 2, "stage_a")
         interleave(2, 2, 4, "stage_b")
-        both_out(1, 3)
         quantize_z(2, 0, 2)
+        project(6, 0)
+        project(6, 1)
+        real_part(6, 1)
+        real_part(6, 0)
+        quantize_set(7)
+        add_imag(6, 0)
         quantize_z(2, 2, 4)
-        for t in range(4):
-            project(6, t)
-            real_part(6, t)
-            add_imag(6, t)
-        interleave(LAST, 0, 2, "stage_a", G_)
+        add_imag(6, 1)
+        project(6, 2)
+        real_part(6, 2)
         expand_pe(2, 0)
         both_out(2, 0)
+        project(6, 3)
+        real_part(6, 3)
+        add_imag(6, 2)
+        add_imag(6, 3)
         expand_pe(2, 1)
-        expand_out(2, 1, 1, V)
-        expand_out(2, 1, 0, V)
+        both_out(2, 1)
+        interleave(LAST, 0, 2, "stage_a")
         project_half(7, 0, 0)
         project_half(7, 1, 0, 0)
         real_part(7, 0)
@@ -512,7 +480,7 @@ def tile_split_real_schrodinger_step_s14_kernel(tc, re, im, phase, v_words, v_sc
         expand_row(LAST, 0)
         expand_row(LAST, 1)
         interleave(LAST, 2, 3, "stage_b")
-        interleave(LAST, 3, 4, "stage_c")
+        interleave(LAST, 3, 4, "stage_a")
         quantize_z(LAST, 2, 3)
         quantize_z(LAST, 3, 4)
         for i in (2, 3):

from contextlib import ExitStack
import math

import concourse.mybir as mybir
from concourse.masks import make_identity

G, M, K, F, N = 4, 512, 1024, 512, 1024
FLOPS = 2 * G * (2 * M * K * F + M * F * N)

F32 = mybir.dt.float32
BF16 = mybir.dt.bfloat16
U32 = mybir.dt.uint32
U16 = mybir.dt.uint16
I32 = mybir.dt.int32
U8 = mybir.dt.uint8
FP8X4 = mybir.dt.float8_e4m3fn_x4
FP4X4 = mybir.dt.float4_e2m1fn_x4
ALU = mybir.AluOpType
ACT = mybir.ActivationFunctionType
P = 128
SETS = 2 * G
LAST = G - 1
BANKS = 8


def tile_split_real_schrodinger_step_s14_kernel(tc, re, im, phase, v_words, v_scales, u_words, u_scales, out):
    nc = tc.nc
    with ExitStack() as ctx:
        keep = ctx.enter_context(tc.tile_pool(name="keep", bufs=1))
        work = ctx.enter_context(tc.tile_pool(name="work", bufs=2))
        psum = ctx.enter_context(tc.psum_pool(name="psum", bufs=1))
        ctx.enter_context(tc.manual_schedule())

        v_raw = [keep.tile([P, 2, 1024], U8, name="v_raw%d" % c, align_bytes=256) for c in range(G)]
        v_dealt = [keep.tile([P, 2, 4, 256], U8, name="v_dealt%d" % c, align_bytes=256) for c in range(G)]
        vs_raw = [keep.tile([P, 2, 512], U8, name="vs_raw0", align_bytes=256), keep.tile([P, 6, 512], U8, name="vs_raw1", align_bytes=256)]
        vs_dealt = [keep.tile([P, 2, 4, 128], U8, name="vs_dealt%d" % c, align_bytes=256) for c in range(G)]
        u_codes = [keep.tile([P, 2048], U8, name="u_codes%d" % c, align_bytes=256) for c in range(G)]
        u_plane = keep.tile([P, G, 1024], U8, name="u_plane", align_bytes=256)
        ident = keep.tile([P, P], F32, name="ident")
        theta = keep.tile([P, G, 4], BF16, name="theta")
        turns = keep.tile([P, 2, 4 * G], F32, name="turns")
        whole = keep.tile([P, 2, 4 * G], I32, name="whole")
        rest = keep.tile([P, 2, 4 * G], F32, name="rest")
        half_sine = keep.tile([P, 2, 4 * G], F32, name="half_sine")
        squared = keep.tile([P, 2, 4 * G], F32, name="squared")
        trig = keep.tile([P, 2, 4 * G], F32, name="trig")

        words = {}
        word_pairs = {}

        def tile_rows(s, q):
            c = s // 2
            if c < LAST:
                return s % 2, q
            return q // 2, 2 * (s % 2) + q % 2

        def load_x(s, q0, q1):
            part, i0 = tile_rows(s, q0)
            xt = keep.tile([P, q1 - q0, K], BF16, name="rows%d_%d" % (s, q0), align_bytes=256)
            rows = (re, im)[part][s // 2].rearrange("(p i) k -> p i k", i=4)
            nc.sync.dma_start(out=xt[:], in_=rows[:, i0 : i0 + q1 - q0, :])
            for q in range(q0, q1):
                words[s, q] = xt[:].bitcast(F32)[:, q - q0, :]
                if q + 1 < q1:
                    word_pairs[s, q] = xt[:].bitcast(F32)[:, q - q0 : q - q0 + 2, :]

        def load_set(s):
            load_x(s, 0, 2)
            load_x(s, 2, 4)

        def load_v(c):
            nc.sync.dma_start(out=v_raw[c][:].bitcast(I32), in_=v_words[2 * c : 2 * c + 2].bitcast(I32).rearrange("g p b -> p g b"))

        def load_u(c):
            nc.sync.dma_start(out=u_codes[c][:].bitcast(I32), in_=u_words[c].bitcast(I32))

        def load_plane(plane, rows):
            for q in range(4):
                nc.sync.dma_start(
                    out=plane[:].bitcast(I32)[32 * q : 32 * q + 4, :, :],
                    in_=rows.bitcast(I32)[:, 4 * q : 4 * q + 4, :].rearrange("g r n -> r g n"),
                )

        nc.scalar.dma_start(out=theta[:], in_=phase.rearrange("c (p t) -> p c t", t=4))
        nc.vector.memset(vs_raw[0][:].bitcast(I32), 0)
        nc.vector.memset(vs_raw[1][:].bitcast(I32), 0)
        make_identity(nc, ident[:])
        nc.vector.memset(u_plane[:].bitcast(I32), 0)

        load_x(0, 0, 1)
        load_x(0, 1, 2)
        load_x(0, 2, 4)
        load_x(1, 0, 2)
        load_plane(vs_raw[0], v_scales[0:2])
        load_v(0)
        load_x(1, 2, 4)
        load_set(2)
        load_set(3)
        load_v(1)
        load_plane(vs_raw[1], v_scales[2:8])
        load_set(4)
        load_u(0)
        load_plane(u_plane, u_scales)
        load_set(5)
        load_v(2)
        load_set(6)
        load_u(1)
        load_set(7)
        load_v(3)
        load_u(2)
        load_u(3)

        theta_flat = theta[:].rearrange("p c t -> p (c t)")

        def trig_reduce():
            for dst in (turns, whole):
                for s in range(2):
                    nc.vector.tensor_scalar(
                        out=dst[:, s, :], in0=theta_flat, scalar1=0.5 / math.pi, scalar2=-0.25 * (1 - s), op0=ALU.mult, op1=ALU.add
                    )
            nc.vector.scalar_tensor_tensor(out=rest[:], in0=whole[:], scalar=-1.0, in1=turns[:], op0=ALU.mult, op1=ALU.add)
            nc.scalar.activation(out=half_sine[:], in_=rest[:], func=ACT.Sin, scale=math.pi)

        def trig_square():
            nc.vector.scalar_tensor_tensor(out=squared[:], in0=half_sine[:], scalar=-2.0, in1=half_sine[:], op0=ALU.mult, op1=ALU.mult)

        def trig_finish():
            nc.vector.tensor_scalar(out=trig[:], in0=squared[:], scalar1=1.0, scalar2=None, op0=ALU.add)

        banks = {}
        taken = []

        def new_bank(key):
            b = psum.tile([P, 512], F32, name="bank%d" % (len(taken) % BANKS))
            taken.append(key)
            banks[key] = b
            return b

        def copy_on(engine, dst, src):
            if engine == "vector":
                nc.vector.tensor_copy(out=dst, in_=src)
            elif engine == "gpsimd":
                nc.gpsimd.tensor_copy(out=dst, in_=src)
            else:
                nc.scalar.copy(out=dst, in_=src)

        sorted_words = {}

        def sort_pair(s, q, engine, slot):
            w = work.tile([P, 2, 512], F32, name=slot, bufs=1, align_bytes=256)
            sorted_words[s, q] = w[:, 0, :]
            sorted_words[s, q + 1] = w[:, 1, :]
            copy_on(
                engine,
                w[:].rearrange("p j (g e b r) -> p (j g) b e r", g=2, e=2, r=8),
                word_pairs[s, q].rearrange("p j (g b r e) -> p (j g) b e r", g=2, e=2, r=8),
            )

        def turn(u, q):
            b = new_bank(("T", u, q))
            for g in range(2):
                for e in range(2):
                    w0 = 256 * g + 128 * e
                    if (u, q) in sorted_words:
                        source = sorted_words[u, q][:, w0 : w0 + 128]
                    else:
                        source = words[u, q][:, 256 * g + e : 256 * (g + 1) : 2]
                    nc.tensor.transpose(b[:, w0 : w0 + 128], source, ident[:])

        grouped = {}
        codes = {}
        scales = {}

        def turn_out(u, q, engine):
            if u not in grouped:
                grouped[u] = work.tile([P, 2, 2048], BF16, name="grouped%d" % (u % 2), bufs=1, align_bytes=256)
                codes[u] = work.tile([P, 2, 512], U32, name="codes%d" % u, bufs=1, align_bytes=256)
                scales[u] = keep.tile([P, 2, 512], U8, name="scales%d" % u, align_bytes=256)
            dst = grouped[u][:].bitcast(F32).rearrange("p g (n e) -> p g n e", e=2)[:, :, 128 * q : 128 * (q + 1), :]
            copy_on(engine, dst, banks["T", u, q][:].rearrange("p (g e r) -> p g r e", g=2, e=2))

        def quantize_set(s):
            nc.vector.quantize_mx(
                out=codes[s][:].rearrange("p g n -> p (g n)").bitcast(FP8X4),
                scales=scales[s][:].rearrange("p g n -> p (g n)"),
                in_=grouped[s][:].rearrange("p g n -> p (g n)"),
            )

        def deal_codes(c, engine="vector", g0=0, g1=2):
            copy_on(
                engine,
                v_dealt[c][:, g0:g1].bitcast(U16).rearrange("p g t (b m) -> p g b t m", m=8),
                v_raw[c][:, g0:g1].bitcast(U16).rearrange("p g (b m t) -> p g b t m", t=4, m=8),
            )

        def deal_scales(c, engine="vector", g0=0, g1=2):
            raw = vs_raw[0][:] if c == 0 else vs_raw[1][:, 2 * (c - 1) : 2 * c, :]
            copy_on(
                engine,
                vs_dealt[c][:, g0:g1].rearrange("p g t (b m) -> p g b t m", m=16),
                raw[:, g0:g1].rearrange("p g (b m t) -> p g b t m", t=4, m=16),
            )

        def project(u, t):
            c = u // 2
            b = new_bank(("AB", u, t))
            for g in range(2):
                nc.tensor.matmul_mx(
                    out=b[:],
                    lhsT=v_dealt[c][:, g, t, :].bitcast(FP4X4),
                    lhsT_scale=vs_dealt[c][:, g, t, :],
                    rhs=codes[u][:, g, :].bitcast(FP8X4),
                    rhs_scale=scales[u][:, g, :],
                    start=(g == 0),
                    stop=(g == 1),
                )

        halves = {}

        def project_half(u, t, part, beside=None):
            c = u // 2
            cols = slice(256 * part, 256 * (part + 1))
            if beside is None:
                halves[u, t, part] = new_bank(("AB", u, t, part))[:, 0:256]
            else:
                halves[u, t, part] = banks["AB", u, beside, part][:, 256:512]
            for g in range(2):
                nc.tensor.matmul_mx(
                    out=halves[u, t, part],
                    lhsT=v_dealt[c][:, g, t, :].bitcast(FP4X4),
                    lhsT_scale=vs_dealt[c][:, g, t, :],
                    rhs=codes[u][:, g, cols].bitcast(FP8X4),
                    rhs_scale=scales[u][:, g, cols],
                    start=(g == 0),
                    stop=(g == 1),
                )

        def amplitudes(s, t, part, cols):
            if (s, t, part) in halves:
                return halves[s, t, part]
            return banks["AB", s, t][:, cols]

        a_cos = {}
        z_rows = {}
        z_grouped = {}
        z_codes = {}
        z_scales = {}

        def amplitude_cols(s):
            if s // 2 < LAST:
                return slice(0, 512), slice(0, 512), slice(0, 512)
            return slice(0, 256), slice(256, 512), slice(256 * (s % 2), 256 * (s % 2 + 1))

        def real_part(s, t, engine="scalar"):
            c = s // 2
            if (c, t) not in a_cos:
                a_cos[c, t] = work.tile([P, 512], F32, name="a_cos", bufs=6)
            a_cols, b_cols, cols = amplitude_cols(s)
            if engine == "vector":
                nc.vector.tensor_scalar(
                    out=a_cos[c, t][:, cols], in0=amplitudes(s, t, 0, a_cols), scalar1=trig[:, 1, 4 * c + t : 4 * c + t + 1], scalar2=None, op0=ALU.mult
                )
            else:
                nc.scalar.activation(
                    out=a_cos[c, t][:, cols], in_=amplitudes(s, t, 0, a_cols), func=ACT.Copy, scale=trig[:, 1, 4 * c + t : 4 * c + t + 1]
                )

        def add_imag(s, t):
            c = s // 2
            if c not in z_rows:
                z_rows[c] = work.tile([P, 4, 512], BF16, name="z_rows", bufs=2)
                z_codes[c] = work.tile([P, 512], U32, name="z_codes", bufs=2, align_bytes=256)
                z_scales[c] = work.tile([P, 512], U8, name="z_scales", bufs=2, align_bytes=256)
            a_cols, b_cols, cols = amplitude_cols(s)
            nc.vector.scalar_tensor_tensor(
                out=z_rows[c][:, t, cols], in0=amplitudes(s, t, 1, b_cols), scalar=trig[:, 0, 4 * c + t : 4 * c + t + 1],
                in1=a_cos[c, t][:, cols], op0=ALU.mult, op1=ALU.add,
            )

        def interleave(c, i0, i1, slot, engine="vector"):
            cols = slice(128 * i0, 128 * i1)
            zt = work.tile([P, 128 * (i1 - i0), 4], BF16, name=slot, bufs=1, align_bytes=256)
            z_grouped[c, i0] = zt
            copy_on(
                engine,
                zt[:].rearrange("p (b n) t -> p b t n", n=4),
                z_rows[c][:, :, cols].rearrange("p t (b n) -> p b t n", n=4),
            )

        def quantize_z(c, i0, i1):
            cols = slice(128 * i0, 128 * i1)
            nc.vector.quantize_mx(
                out=z_codes[c][:, cols].bitcast(FP8X4), scales=z_scales[c][:, cols],
                in_=z_grouped[c, i0][:].rearrange("p n t -> p (n t)"),
            )

        def expand(c, i, n):
            cols = slice(128 * i, 128 * (i + 1))
            b = new_bank(("O", c, i, n))
            nc.tensor.matmul_mx(
                out=b[:],
                lhsT=z_codes[c][:, cols].bitcast(FP8X4),
                lhsT_scale=z_scales[c][:, cols],
                rhs=u_codes[c][:, 1024 * n : 1024 * (n + 1)].bitcast(FP4X4),
                rhs_scale=u_plane[:, c, 512 * n : 512 * (n + 1)],
                start=True,
                stop=True,
            )

        out_rows = {}
        out_slots = ["out%d" % j for j in range(4)] + ["codes%d" % j for j in range(6)] + ["sorted%d" % j for j in range(4)] + ["grouped0", "grouped1"]
        copied = []

        def expand_out(c, i, n, engine):
            if (c, i) not in out_rows:
                out_rows[c, i] = work.tile([P, 1024], F32, name=out_slots[4 * c + i], bufs=1, align_bytes=256)
            cols = slice(512 * n, 512 * (n + 1))
            copy_on(engine, out_rows[c, i][:, cols], banks["O", c, i, n][:])
            copied.append((c, i, n))
            dst = out[c].rearrange("(p i) n -> p i n", i=4)[:, i, :]
            if c == LAST and i == 3:
                nc.sync.dma_start(out=dst[:, cols], in_=out_rows[c, i][:, cols])
            elif (c, i, 1 - n) in copied:
                nc.sync.dma_start(out=dst, in_=out_rows[c, i][:])

        S, V = "scalar", "vector"

        def turn_pair(s, q, first=S, second=S):
            turn(s, q)
            turn(s, q + 1)
            turn_out(s, q + 1, first)
            turn_out(s, q, second)

        def expand_row(c, i, first=S, second=S):
            expand(c, i, 0)
            expand(c, i, 1)
            expand_out(c, i, 1, first)
            expand_out(c, i, 0, second)

        def real_modes(c, t):
            project(2 * c, t)

        def imag_modes(c, t):
            project(2 * c + 1, t)

        def expand_pe(c, i):
            expand(c, i, 0)
            expand(c, i, 1)

        def both_out(c, i):
            expand_out(c, i, 1, S)
            expand_out(c, i, 0, S)

        trig_reduce()
        turn(0, 0)
        turn_out(0, 0, S)
        trig_square()
        turn(0, 1)
        turn_out(0, 1, S)
        trig_finish()
        turn_pair(0, 2, S, V)
        deal_scales(0)
        quantize_set(0)
        deal_codes(0)
        turn_pair(1, 0)
        turn_pair(1, 2)
        sort_pair(2, 0, V, "sorted0")

        real_modes(0, 0)
        real_modes(0, 1)
        sort_pair(2, 2, V, "sorted1")
        quantize_set(1)
        real_part(0, 0)
        real_part(0, 1)
        turn_pair(2, 0)
        sort_pair(3, 0, V, "sorted2")
        real_modes(0, 2)
        real_modes(0, 3)
        real_part(0, 3)
        real_part(0, 2)
        sort_pair(3, 2, V, "sorted3")
        turn_pair(2, 2)
        deal_codes(1)
        deal_scales(1)
        imag_modes(0, 0)
        imag_modes(0, 1)
        add_imag(1, 0)
        quantize_set(2)
        add_imag(1, 1)
        turn_pair(3, 0)
        imag_modes(0, 2)
        add_imag(1, 2)
        imag_modes(0, 3)
        add_imag(1, 3)
        turn_pair(3, 2)

        for c in (1, 2):
            p = c - 1
            interleave(p, 0, 2, "stage_a")
            interleave(p, 2, 4, "stage_b")
            quantize_z(p, 0, 2)
            real_modes(c, 0)
            real_modes(c, 1)
            real_part(2 * c, 1)
            real_part(2 * c, 0)
            quantize_set(2 * c + 1)
            quantize_z(p, 2, 4)
            turn_pair(2 * c + 2, 0)
            if c == 1:
                sort_pair(5, 0, V, "sorted0")
            real_modes(c, 2)
            real_modes(c, 3)
            real_part(2 * c, 3)
            real_part(2 * c, 2)
            expand_pe(p, 0)
            expand_out(p, 0, 1, V)
            expand_out(p, 0, 0, V)
            deal_codes(c + 1)
            turn_pair(2 * c + 2, 2)
            expand_pe(p, 1)
            both_out(p, 1)
            imag_modes(c, 0)
            imag_modes(c, 1)
            deal_scales(c + 1)
            add_imag(2 * c + 1, 1)
            add_imag(2 * c + 1, 0)
            quantize_set(2 * c + 2)
            turn_pair(2 * c + 3, 0)
            imag_modes(c, 2)
            add_imag(2 * c + 1, 2)
            expand_pe(p, 2)
            both_out(p, 2)
            imag_modes(c, 3)
            add_imag(2 * c + 1, 3)
            expand_pe(p, 3)
            both_out(p, 3)
            turn_pair(2 * c + 3, 2)

        interleave(2, 0, 2, "stage_a")
        interleave(2, 2, 4, "stage_b")
        quantize_z(2, 0, 2)
        project(6, 0)
        project(6, 1)
        real_part(6, 1)
        real_part(6, 0)
        quantize_set(7)
        add_imag(6, 0)
        quantize_z(2, 2, 4)
        add_imag(6, 1)
        project(6, 2)
        real_part(6, 2)
        expand_pe(2, 0)
        both_out(2, 0)
        project(6, 3)
        real_part(6, 3)
        add_imag(6, 2)
        add_imag(6, 3)
        expand_pe(2, 1)
        both_out(2, 1)
        interleave(LAST, 0, 2, "stage_a")
        project_half(7, 0, 0)
        project_half(7, 1, 0, 0)
        real_part(7, 0)
        real_part(7, 1)
        expand_pe(2, 2)
        expand_out(2, 2, 1, S)
        expand_out(2, 2, 0, V)
        quantize_z(LAST, 0, 2)
        project_half(7, 2, 0)
        project_half(7, 3, 0, 2)
        real_part(7, 2)
        real_part(7, 3)
        expand_pe(2, 3)
        both_out(2, 3)
        for t in range(4):
            project_half(7, t, 1)
            add_imag(7, t)

        expand_row(LAST, 0)
        expand_row(LAST, 1)
        interleave(LAST, 2, 3, "stage_b")
        interleave(LAST, 3, 4, "stage_a")
        quantize_z(LAST, 2, 3)
        quantize_z(LAST, 3, 4)
        for i in (2, 3):
            for n in range(2):
                expand(LAST, i, n)
                expand_out(LAST, i, n, (V, S)[n])
